import numpy as np
import ml_dtypes


def mxq(x, axis, fmt="e4m3"):
    dtype, down = {"e4m3": (ml_dtypes.float8_e4m3fn, 7), "e5m2": (ml_dtypes.float8_e5m2, 14)}[fmt]
    v = np.moveaxis(np.asarray(x, np.float32).astype(ml_dtypes.bfloat16).astype(np.float64), axis, -1)
    blocks = v.reshape(v.shape[:-1] + (-1, 32))
    amax = np.abs(blocks).max(-1, keepdims=True)
    byte = np.maximum(np.where(amax > 0, np.frexp(amax)[1] - 1 + 127, 0) - down, 1)
    scale = np.exp2(byte - 127.0)
    codes = (blocks / scale).astype(np.float32).astype(dtype).astype(np.float64)
    return np.moveaxis((codes * scale).reshape(v.shape), -1, axis)


WIDE = False


def mx_kscale(k):
    if not WIDE:
        return np.ones(k)
    levels = np.array([10, -10, 5, -5, 0])
    if k % 512:
        return np.exp2(np.random.permutation(np.resize(levels, k // 32))).repeat(32)
    a = np.empty((k // 512, 16))
    for p in range(k // 512):
        a[p, :8] = np.random.permutation(np.resize(levels, 8))
        for g in range(8):
            far = levels[np.abs(levels - a[p, g]) >= 10]
            a[p, g + 8] = far[np.random.randint(len(far))]
    return np.exp2(a.ravel()).repeat(32)


def f64(x):
    return np.asarray(x).astype(np.float64)


def striped(idx):
    return np.tile(idx.reshape(-1, 16).T, (8, 1)).astype(np.uint16)


def unstriped(offs):
    return offs[:16].T.reshape(-1).astype(np.int64)


def sigmoid(v):
    return 1.0 / (1.0 + np.exp(-np.maximum(v, -700.0)))


K, T, S, V, N = 512, 4096, 1536, 384, 256


def setup_inputs():
    n = np.random.standard_normal
    s = mx_kscale(K)[:, None]
    return {
        "xT": (n((K, T)) * s).astype(np.float32),
        "w1": (n((K, N)) / np.sqrt(K) / s).astype(np.float32),
        "offs": striped(np.random.permutation(T)[:S]),
    }


def reference(xT, w1, offs):
    xq = mxq(f64(xT)[:, unstriped(offs)], 0, "e4m3")
    y = sigmoid(mxq(f64(w1), 0, "e4m3").T @ xq)
    return ((y[:, :V] * y[:, V:2 * V]) * y[:, 2 * V:3 * V]) * y[:, 3 * V:4 * V]

@@ -1,0 +1,145 @@
+from contextlib import ExitStack
+
+import concourse.mybir as mybir
+
+K, T, S, V, N = 512, 4096, 1536, 384, 256
+FLOPS = 2 * K * S * N
+
+F32 = mybir.dt.float32
+BF16 = mybir.dt.bfloat16
+U32 = mybir.dt.uint32
+U16 = mybir.dt.uint16
+U8 = mybir.dt.uint8
+FP8X4 = mybir.dt.float8_e4m3fn_x4
+SIGMOID = mybir.ActivationFunctionType.Sigmoid
+MULT = mybir.AluOpType.mult
+
+P = 128
+PACK = 4
+SL = 512
+BLK = 128
+MT = N // P
+
+
+def tile_picked_andpool_none_e_kernel(tc, xT, w1, offs, out):
+    nc = tc.nc
+    with ExitStack() as ctx:
+        keep = ctx.enter_context(tc.tile_pool(name="keep", bufs=1))
+        psum = ctx.enter_context(tc.psum_pool(name="psum", bufs=1))
+
+        offsets = keep.tile([P, S // 16], U16, name="offsets")
+        planes = [keep.tile([P, T], F32, name=f"plane{j}") for j in range(PACK)]
+        w_raw = keep.tile([P, PACK, N], F32, name="w_raw", tag="shared", align_bytes=64)
+        x_rows = xT.rearrange("(p j) t -> p j t", j=PACK)
+        nc.sync.dma_start(offsets[:], offs)
+        for j in range(PACK):
+            nc.sync.dma_start(out=planes[j][:], in_=x_rows[:, j, :])
+        nc.sync.dma_start(out=w_raw[:], in_=w1.rearrange("(p j) m -> p j m", j=PACK))
+
+        warm_in = keep.tile([P, 1], F32, name="warm_in")
+        warm_out = keep.tile([P, 1], F32, name="warm_out")
+        nc.gpsimd.memset(warm_in[:], 0.0)
+        nc.scalar.activation(warm_out[:], warm_in[:], SIGMOID)
+
+        grouped = [keep.tile([P, SL, PACK], BF16, name=f"grouped{s}", align_bytes=64) for s in range(3)]
+        staged = [keep.tile([P, PACK, SL], F32, name=f"staged{s}") for s in range(3)]
+
+        def window(j, s):
+            return planes[j][:].indirect(offsets[:, s * SL // 16:(s + 1) * SL // 16])
+
+        def gather(j, s):
+            nc.vector.tensor_copy(staged[s][:, j, :], window(j, s))
+
+        def gather_in_place(j, s):
+            nc.vector.tensor_copy(grouped[s][:, :, j], window(j, s))
+
+        def weave(s, j0, j1):
+            nc.scalar.copy(grouped[s][:, :, j0:j1], staged[s][:, j0:j1, :].rearrange("p j s -> p s j"))
+
+        w_grouped = keep.tile([P, N, PACK], BF16, name="w_grouped", align_bytes=64)
+        w_codes = keep.tile([P, N], U32, name="w_codes", align_bytes=64)
+        w_scales = keep.tile([P, N], U8, name="w_scales", align_bytes=64)
+        scales = keep.tile([P, S], U8, name="scales", align_bytes=64)
+
+        def weave_w():
+            nc.scalar.copy(w_grouped[:], w_raw[:].rearrange("p j m -> p m j"))
+
+        def quant_w():
+            nc.vector.quantize_mx(out=w_codes[:].bitcast(FP8X4), scales=w_scales[:], in_=w_grouped[:].rearrange("p m j -> p (m j)"))
+
+        truth = {}
+        codes = {}
+
+        def quant(b0, nb):
+            s, c0, n = b0 * BLK // SL, b0 * BLK % SL, nb * BLK
+            cols = slice(b0 * BLK, b0 * BLK + n)
+            nc.vector.quantize_mx(out=codes[0][:, cols].bitcast(FP8X4), scales=scales[:, cols], in_=grouped[s][:, c0:c0 + n, :].rearrange("p s j -> p (s j)"))
+
+        def product(b0, nb):
+            n = nb * BLK
+            cols = slice(b0 * BLK, b0 * BLK + n)
+            bank = psum.tile([P, MT, n], F32, name=f"bank{b0}")
+            for m in range(MT):
+                nc.tensor.matmul_mx(out=bank[:, m, :], lhsT=w_codes[:, m * P:(m + 1) * P].bitcast(FP8X4), lhsT_scale=w_scales[:, m * P:(m + 1) * P],
+                                    rhs=codes[0][:, cols].bitcast(FP8X4), rhs_scale=scales[:, cols], start=True, stop=True)
+            y = keep.tile([P, nb, MT, BLK], F32, name=f"truth{b0}")
+            nc.scalar.activation(y[:], bank[:].rearrange("p m (b v) -> p b m v", b=nb), SIGMOID)
+            for b in range(nb):
+                truth[b0 + b] = y[:, b]
+
+        def times(name, a, b):
+            r = keep.tile([P, MT, BLK], F32, name=name)
+            nc.vector.tensor_tensor(r[:], a, b, MULT)
+            return r[:]
+
+        out_v = out.rearrange("(m p) v -> p m v", p=P)
+
+        def store(engine, c, r):
+            engine.dma_start(out=out_v[:, :, c * BLK:(c + 1) * BLK], in_=r)
+
+        def weave_twice(s, j):
+            nc.scalar.copy(grouped[s][:, :, j:j + 2], staged[s][:, j:j + 1, :].rearrange("p j s -> p s j").to_broadcast([P, SL, 2]))
+
+        for s in (1, 2, 0):
+            gather(0, s)
+        for s in (1, 2, 0):
+            gather(1, s)
+            weave(s, 0, 2)
+        for s in (1, 2):
+            gather(2, s)
+            weave_twice(s, 2)
+        gather(2, 0)
+
+        gather(3, 0)
+        weave_w()
+        weave(0, 2, 4)
+        gather_in_place(3, 1)
+        gather_in_place(3, 2)
+        quant_w()
+        codes[0] = keep.tile([P, S], U32, name="codes", tag="shared", align_bytes=64)
+        quant(4, 1)
+        product(4, 1)
+        quant(5, 1)
+        product(5, 1)
+        quant(6, 2)
+        product(6, 2)
+        quant(0, 4)
+        product(0, 2)
+        product(2, 2)
+        quant(8, 4)
+        product(8, 2)
+        product(10, 1)
+        product(11, 1)
+
+        p47 = times("p47", truth[4], truth[7])
+        p06 = times("p06", truth[0], truth[6])
+        p147 = times("p147", truth[1], p47)
+        p25 = times("p25", truth[2], truth[5])
+        p036 = times("p036", truth[3], p06)
+        p258 = times("p258", truth[8], p25)
+        r0 = times("r0", truth[9], p036)
+        store(nc.sync, 0, r0)
+        r1 = times("r1", truth[10], p147)
+        store(nc.sync, 1, r1)
+        r2 = times("r2", truth[11], p258)
+        store(nc.scalar, 2, r2)

@@ -31,9 +31,10 @@ def tile_picked_andpool_none_e_kernel(tc, xT, w1, offs, out):
         planes = [keep.tile([P, T], F32, name=f"plane{j}") for j in range(PACK)]
         w_raw = keep.tile([P, PACK, N], F32, name="w_raw", tag="shared", align_bytes=64)
         x_rows = xT.rearrange("(p j) t -> p j t", j=PACK)
-        nc.sync.dma_start(offsets[:], offs)
         for j in range(PACK):
             nc.sync.dma_start(out=planes[j][:], in_=x_rows[:, j, :])
+            if j == 0:
+                nc.sync.dma_start(offsets[:], offs)
         nc.sync.dma_start(out=w_raw[:], in_=w1.rearrange("(p j) m -> p j m", j=PACK))
 
         warm_in = keep.tile([P, 1], F32, name="warm_in")
@@ -42,7 +43,7 @@ def tile_picked_andpool_none_e_kernel(tc, xT, w1, offs, out):
         nc.scalar.activation(warm_out[:], warm_in[:], SIGMOID)
 
         grouped = [keep.tile([P, SL, PACK], BF16, name=f"grouped{s}", align_bytes=64) for s in range(3)]
-        staged = [keep.tile([P, PACK, SL], F32, name=f"staged{s}") for s in range(3)]
+        staged = [keep.tile([P, PACK, SL], F32, name=f"staged{s}") for s in range(2)]
 
         def window(j, s):
             return planes[j][:].indirect(offsets[:, s * SL // 16:(s + 1) * SL // 16])
@@ -100,15 +101,17 @@ def tile_picked_andpool_none_e_kernel(tc, xT, w1, offs, out):
         def weave_twice(s, j):
             nc.scalar.copy(grouped[s][:, :, j:j + 2], staged[s][:, j:j + 1, :].rearrange("p j s -> p s j").to_broadcast([P, SL, 2]))
 
-        for s in (1, 2, 0):
+        for s in (1, 0):
             gather(0, s)
-        for s in (1, 2, 0):
+        gather_in_place(0, 2)
+        for s in (1, 0):
             gather(1, s)
             weave(s, 0, 2)
-        for s in (1, 2):
-            gather(2, s)
-            weave_twice(s, 2)
+        gather_in_place(1, 2)
+        gather(2, 1)
+        weave_twice(1, 2)
         gather(2, 0)
+        gather_in_place(2, 2)
 
         gather(3, 0)
         weave_w()

@@ -63,7 +63,7 @@ def tile_picked_andpool_none_e_kernel(tc, xT, w1, offs, out):
         scales = keep.tile([P, S], U8, name="scales", align_bytes=64)
 
         def weave_w():
-            nc.scalar.copy(w_grouped[:], w_raw[:].rearrange("p j m -> p m j"))
+            nc.gpsimd.tensor_scalar(w_grouped[:], w_raw[:].rearrange("p j m -> p m j"), 1.0, 0.0, MULT, mybir.AluOpType.add)
 
         def quant_w():
             nc.vector.quantize_mx(out=w_codes[:].bitcast(FP8X4), scales=w_scales[:], in_=w_grouped[:].rearrange("p m j -> p (m j)"))
@@ -79,7 +79,7 @@ def tile_picked_andpool_none_e_kernel(tc, xT, w1, offs, out):
         def product(b0, nb):
             n = nb * BLK
             cols = slice(b0 * BLK, b0 * BLK + n)
-            bank = psum.tile([P, MT, n], F32, name=f"bank{b0}")
+            bank = psum.tile([P, MT, n], F32, name="bank", bufs=8)
             for m in range(MT):
                 nc.tensor.matmul_mx(out=bank[:, m, :], lhsT=w_codes[:, m * P:(m + 1) * P].bitcast(FP8X4), lhsT_scale=w_scales[:, m * P:(m + 1) * P],
                                     rhs=codes[0][:, cols].bitcast(FP8X4), rhs_scale=scales[:, cols], start=True, stop=True)
@@ -98,51 +98,38 @@ def tile_picked_andpool_none_e_kernel(tc, xT, w1, offs, out):
         def store(engine, c, r):
             engine.dma_start(out=out_v[:, :, c * BLK:(c + 1) * BLK], in_=r)
 
-        def weave_twice(s, j):
-            nc.scalar.copy(grouped[s][:, :, j:j + 2], staged[s][:, j:j + 1, :].rearrange("p j s -> p s j").to_broadcast([P, SL, 2]))
-
-        for s in (1, 0):
-            gather(0, s)
-        gather_in_place(0, 2)
-        for s in (1, 0):
-            gather(1, s)
-            weave(s, 0, 2)
-        gather_in_place(1, 2)
-        gather(2, 1)
-        weave_twice(1, 2)
-        gather(2, 0)
-        gather_in_place(2, 2)
-
-        gather(3, 0)
+        for j in range(PACK):
+            for s in (0, 1):
+                gather(j, s)
+                if j % 2 == 1:
+                    weave(s, j - 1, j + 1)
+            gather_in_place(j, 2)
         weave_w()
-        weave(0, 2, 4)
-        gather_in_place(3, 1)
-        gather_in_place(3, 2)
         quant_w()
         codes[0] = keep.tile([P, S], U32, name="codes", tag="shared", align_bytes=64)
-        quant(4, 1)
-        product(4, 1)
-        quant(5, 1)
-        product(5, 1)
-        quant(6, 2)
-        product(6, 2)
-        quant(0, 4)
-        product(0, 2)
-        product(2, 2)
-        quant(8, 4)
+        quant(0, 1)
+        product(0, 1)
+        quant(3, 1)
+        product(3, 1)
+        quant(8, 2)
         product(8, 2)
-        product(10, 1)
-        product(11, 1)
-
-        p47 = times("p47", truth[4], truth[7])
-        p06 = times("p06", truth[0], truth[6])
-        p147 = times("p147", truth[1], p47)
-        p25 = times("p25", truth[2], truth[5])
-        p036 = times("p036", truth[3], p06)
-        p258 = times("p258", truth[8], p25)
-        r0 = times("r0", truth[9], p036)
+        quant(10, 2)
+        product(10, 2)
+        quant(1, 2)
+        product(2, 1)
+        product(1, 1)
+        quant(4, 4)
+        for b in (4, 5, 6, 7):
+            product(b, 1)
+        p03 = times("p03", truth[0], truth[3])
+        p039 = times("p039", truth[9], p03)
+        p8b = times("p8b", truth[8], truth[11])
+        p28b = times("p28b", truth[2], p8b)
+        p1a = times("p1a", truth[1], truth[10])
+        p14a = times("p14a", truth[4], p1a)
+        r2 = times("r2", truth[5], p28b)
+        store(nc.sync, 2, r2)
+        r0 = times("r0", truth[6], p039)
         store(nc.sync, 0, r0)
-        r1 = times("r1", truth[10], p147)
-        store(nc.sync, 1, r1)
-        r2 = times("r2", truth[11], p258)
-        store(nc.scalar, 2, r2)
+        r1 = times("r1", truth[7], p14a)
+        store(nc.scalar, 1, r1)

@@ -12,13 +12,18 @@ U16 = mybir.dt.uint16
 U8 = mybir.dt.uint8
 FP8X4 = mybir.dt.float8_e4m3fn_x4
 SIGMOID = mybir.ActivationFunctionType.Sigmoid
+COPY = mybir.ActivationFunctionType.Copy
 MULT = mybir.AluOpType.mult
+ADD = mybir.AluOpType.add
 
 P = 128
 PACK = 4
 SL = 512
 BLK = 128
 MT = N // P
+
+CHUNKS = (1728, 1152, 704, 512)
+GPSIMD_SHARE = (1280, 512, 320, 256)
 
 
 def tile_picked_andpool_none_e_kernel(tc, xT, w1, offs, out):
@@ -29,12 +34,16 @@ def tile_picked_andpool_none_e_kernel(tc, xT, w1, offs, out):
 
         offsets = keep.tile([P, S // 16], U16, name="offsets")
         planes = [keep.tile([P, T], F32, name=f"plane{j}") for j in range(PACK)]
+        last_bf = keep.tile([P, T], BF16, name="last_bf")
         w_raw = keep.tile([P, PACK, N], F32, name="w_raw", tag="shared", align_bytes=64)
         x_rows = xT.rearrange("(p j) t -> p j t", j=PACK)
-        for j in range(PACK):
-            nc.sync.dma_start(out=planes[j][:], in_=x_rows[:, j, :])
-            if j == 0:
-                nc.sync.dma_start(offsets[:], offs)
+        nc.sync.dma_start(out=planes[2][:], in_=x_rows[:, 2, :])
+        nc.sync.dma_start(offsets[:], offs)
+        nc.sync.dma_start(out=planes[0][:], in_=x_rows[:, 0, :])
+        nc.sync.dma_start(out=planes[1][:], in_=x_rows[:, 1, :])
+        starts = [sum(CHUNKS[:i]) for i in range(len(CHUNKS) + 1)]
+        for i in range(len(CHUNKS)):
+            nc.sync.dma_start(out=planes[3][:, starts[i]:starts[i + 1]], in_=x_rows[:, 3, starts[i]:starts[i + 1]])
         nc.sync.dma_start(out=w_raw[:], in_=w1.rearrange("(p j) m -> p j m", j=PACK))
 
         warm_in = keep.tile([P, 1], F32, name="warm_in")
@@ -43,93 +52,76 @@ def tile_picked_andpool_none_e_kernel(tc, xT, w1, offs, out):
         nc.scalar.activation(warm_out[:], warm_in[:], SIGMOID)
 
         grouped = [keep.tile([P, SL, PACK], BF16, name=f"grouped{s}", align_bytes=64) for s in range(3)]
-        staged = [keep.tile([P, PACK, SL], F32, name=f"staged{s}") for s in range(2)]
+        pair = keep.tile([P, 2, SL], F32, name="pair")
+        third = [keep.tile([P, SL], F32, name=f"third{s}") for s in (1, 2)]
 
-        def window(j, s):
-            return planes[j][:].indirect(offsets[:, s * SL // 16:(s + 1) * SL // 16])
-
-        def gather(j, s):
-            nc.vector.tensor_copy(staged[s][:, j, :], window(j, s))
+        def entries(s):
+            return offsets[:, s * SL // 16:(s + 1) * SL // 16]
 
         def gather_in_place(j, s):
-            nc.vector.tensor_copy(grouped[s][:, :, j], window(j, s))
+            nc.vector.tensor_copy(grouped[s][:, :, j], planes[j][:].indirect(entries(s)))
 
-        def weave(s, j0, j1):
-            nc.scalar.copy(grouped[s][:, :, j0:j1], staged[s][:, j0:j1, :].rearrange("p j s -> p s j"))
+        def cast_gpsimd(a, b):
+            nc.gpsimd.tensor_scalar(last_bf[:, a:b], planes[3][:, a:b], 1.0, 0.0, MULT, ADD)
+
+        def cast_scalar(a, b):
+            nc.scalar.copy(last_bf[:, a:b], planes[3][:, a:b])
+
+        for s in (1, 2):
+            nc.vector.tensor_copy(third[s - 1][:], planes[2][:].indirect(entries(s)))
+            nc.scalar.copy(grouped[s][:, :, 2], third[s - 1][:])
+        gather_in_place(2, 0)
+        for j in (0, 1):
+            nc.vector.tensor_copy(pair[:, j, :], planes[j][:].indirect(entries(0)))
+            gather_in_place(j, 1)
+            gather_in_place(j, 2)
+        nc.scalar.copy(grouped[0][:, :, 0:2], pair[:].rearrange("p j s -> p s j"))
+        for i in range(len(CHUNKS)):
+            cast_gpsimd(starts[i], starts[i] + GPSIMD_SHARE[i])
+            cast_scalar(starts[i] + GPSIMD_SHARE[i], starts[i + 1])
+        gather_in_place(3, 0)
+        for s in (1, 2):
+            nc.scalar.activation(grouped[s][:, :, 3], last_bf[:].indirect(entries(s)), COPY)
 
         w_grouped = keep.tile([P, N, PACK], BF16, name="w_grouped", align_bytes=64)
         w_codes = keep.tile([P, N], U32, name="w_codes", align_bytes=64)
         w_scales = keep.tile([P, N], U8, name="w_scales", align_bytes=64)
-        scales = keep.tile([P, S], U8, name="scales", align_bytes=64)
+        nc.gpsimd.tensor_scalar(w_grouped[:], w_raw[:].rearrange("p j m -> p m j"), 1.0, 0.0, MULT, ADD)
 
-        def weave_w():
-            nc.gpsimd.tensor_scalar(w_grouped[:], w_raw[:].rearrange("p j m -> p m j"), 1.0, 0.0, MULT, mybir.AluOpType.add)
-
-        def quant_w():
-            nc.vector.quantize_mx(out=w_codes[:].bitcast(FP8X4), scales=w_scales[:], in_=w_grouped[:].rearrange("p m j -> p (m j)"))
-
-        truth = {}
+        scales = [keep.tile([P, SL], U8, name=f"scales{s}", align_bytes=64) for s in range(3)]
         codes = {}
 
-        def quant(b0, nb):
-            s, c0, n = b0 * BLK // SL, b0 * BLK % SL, nb * BLK
-            cols = slice(b0 * BLK, b0 * BLK + n)
-            nc.vector.quantize_mx(out=codes[0][:, cols].bitcast(FP8X4), scales=scales[:, cols], in_=grouped[s][:, c0:c0 + n, :].rearrange("p s j -> p (s j)"))
+        def quant(s):
+            nc.vector.quantize_mx(out=codes[s].bitcast(FP8X4), scales=scales[s][:], in_=grouped[s][:].rearrange("p s j -> p (s j)"))
 
-        def product(b0, nb):
-            n = nb * BLK
-            cols = slice(b0 * BLK, b0 * BLK + n)
-            bank = psum.tile([P, MT, n], F32, name="bank", bufs=8)
+        def truth(d, m):
+            bank = psum.tile([P, V], F32, name=f"bank{d}{m}")
+            lo, hi = d * V, (d + 1) * V
+            cut = lo + 2 * BLK if (lo + 2 * BLK - 1) // SL == lo // SL else lo + BLK
+            for a, b in ((lo, cut), (cut, hi)):
+                s, cols = a // SL, slice(a % SL, a % SL + b - a)
+                nc.tensor.matmul_mx(out=bank[:, a - lo:b - lo], lhsT=w_codes[:, m * P:(m + 1) * P].bitcast(FP8X4), lhsT_scale=w_scales[:, m * P:(m + 1) * P],
+                                    rhs=codes[s][:, cols].bitcast(FP8X4), rhs_scale=scales[s][:, cols], start=True, stop=True)
+            y = keep.tile([P, V], F32, name=f"truth{d}{m}")
+            nc.scalar.activation(y[:], bank[:], SIGMOID)
+            return y
+
+        codes0 = keep.tile([P, SL], U32, name="codes0", align_bytes=64)
+        codes[0] = codes0[:]
+        quant(0)
+        nc.vector.quantize_mx(out=w_codes[:].bitcast(FP8X4), scales=w_scales[:], in_=w_grouped[:].rearrange("p m j -> p (m j)"))
+        codes12 = keep.tile([P, 2 * SL], U32, name="codes12", tag="shared", align_bytes=64)
+        codes[1] = codes12[:, 0:SL]
+        codes[2] = codes12[:, SL:2 * SL]
+        quant(1)
+        quant(2)
+
+        acc = [truth(0, m) for m in range(MT)]
+        for d in range(1, 4):
             for m in range(MT):
-                nc.tensor.matmul_mx(out=bank[:, m, :], lhsT=w_codes[:, m * P:(m + 1) * P].bitcast(FP8X4), lhsT_scale=w_scales[:, m * P:(m + 1) * P],
-                                    rhs=codes[0][:, cols].bitcast(FP8X4), rhs_scale=scales[:, cols], start=True, stop=True)
-            y = keep.tile([P, nb, MT, BLK], F32, name=f"truth{b0}")
-            nc.scalar.activation(y[:], bank[:].rearrange("p m (b v) -> p b m v", b=nb), SIGMOID)
-            for b in range(nb):
-                truth[b0 + b] = y[:, b]
-
-        def times(name, a, b):
-            r = keep.tile([P, MT, BLK], F32, name=name)
-            nc.vector.tensor_tensor(r[:], a, b, MULT)
-            return r[:]
-
-        out_v = out.rearrange("(m p) v -> p m v", p=P)
-
-        def store(engine, c, r):
-            engine.dma_start(out=out_v[:, :, c * BLK:(c + 1) * BLK], in_=r)
-
-        for j in range(PACK):
-            for s in (0, 1):
-                gather(j, s)
-                if j % 2 == 1:
-                    weave(s, j - 1, j + 1)
-            gather_in_place(j, 2)
-        weave_w()
-        quant_w()
-        codes[0] = keep.tile([P, S], U32, name="codes", tag="shared", align_bytes=64)
-        quant(0, 1)
-        product(0, 1)
-        quant(3, 1)
-        product(3, 1)
-        quant(8, 2)
-        product(8, 2)
-        quant(10, 2)
-        product(10, 2)
-        quant(1, 2)
-        product(2, 1)
-        product(1, 1)
-        quant(4, 4)
-        for b in (4, 5, 6, 7):
-            product(b, 1)
-        p03 = times("p03", truth[0], truth[3])
-        p039 = times("p039", truth[9], p03)
-        p8b = times("p8b", truth[8], truth[11])
-        p28b = times("p28b", truth[2], p8b)
-        p1a = times("p1a", truth[1], truth[10])
-        p14a = times("p14a", truth[4], p1a)
-        r2 = times("r2", truth[5], p28b)
-        store(nc.sync, 2, r2)
-        r0 = times("r0", truth[6], p039)
-        store(nc.sync, 0, r0)
-        r1 = times("r1", truth[7], p14a)
-        store(nc.scalar, 1, r1)
+                y = truth(d, m)
+                r = keep.tile([P, V], F32, name=f"prod{d}{m}")
+                nc.vector.tensor_tensor(r[:], acc[m][:], y[:], MULT)
+                acc[m] = r
+                if d == 3:
+                    nc.sync.dma_start(out=out[m * P:(m + 1) * P, :], in_=r[:])

@@ -22,8 +22,11 @@ SL = 512
 BLK = 128
 MT = N // P
 
-CHUNKS = (1728, 1152, 704, 512)
-GPSIMD_SHARE = (1280, 512, 320, 256)
+CHUNKS = (1344, 1152, 832, 512, 256)
+GPSIMD_SHARE = (960, 512, 352, 192, 0)
+VECTOR_SHARE = (0, 0, 0, 0, 0)
+NV = 640
+WOVEN = 512
 
 
 def tile_picked_andpool_none_e_kernel(tc, xT, w1, offs, out):
@@ -35,7 +38,7 @@ def tile_picked_andpool_none_e_kernel(tc, xT, w1, offs, out):
         offsets = keep.tile([P, S // 16], U16, name="offsets")
         planes = [keep.tile([P, T], F32, name=f"plane{j}") for j in range(PACK)]
         last_bf = keep.tile([P, T], BF16, name="last_bf")
-        w_raw = keep.tile([P, PACK, N], F32, name="w_raw", tag="shared", align_bytes=64)
+        w_raw = [keep.tile([P, PACK, P], F32, name=f"w_raw{m}", tag=f"shared{m}", align_bytes=64) for m in range(MT)]
         x_rows = xT.rearrange("(p j) t -> p j t", j=PACK)
         nc.sync.dma_start(out=planes[2][:], in_=x_rows[:, 2, :])
         nc.sync.dma_start(offsets[:], offs)
@@ -44,84 +47,95 @@ def tile_picked_andpool_none_e_kernel(tc, xT, w1, offs, out):
         starts = [sum(CHUNKS[:i]) for i in range(len(CHUNKS) + 1)]
         for i in range(len(CHUNKS)):
             nc.sync.dma_start(out=planes[3][:, starts[i]:starts[i + 1]], in_=x_rows[:, 3, starts[i]:starts[i + 1]])
-        nc.sync.dma_start(out=w_raw[:], in_=w1.rearrange("(p j) m -> p j m", j=PACK))
+        w_rows = w1.rearrange("(p j) m -> p j m", j=PACK)
+        for m in range(MT):
+            nc.sync.dma_start(out=w_raw[m][:], in_=w_rows[:, :, m * P:(m + 1) * P])
 
         warm_in = keep.tile([P, 1], F32, name="warm_in")
         warm_out = keep.tile([P, 1], F32, name="warm_out")
         nc.gpsimd.memset(warm_in[:], 0.0)
         nc.scalar.activation(warm_out[:], warm_in[:], SIGMOID)
 
-        grouped = [keep.tile([P, SL, PACK], BF16, name=f"grouped{s}", align_bytes=64) for s in range(3)]
-        pair = keep.tile([P, 2, SL], F32, name="pair")
-        third = [keep.tile([P, SL], F32, name=f"third{s}") for s in (1, 2)]
+        grouped = keep.tile([P, S, PACK], BF16, name="grouped", align_bytes=64)
+        pair = [keep.tile([P, 2, WOVEN // 2], BF16, name=f"pair{h}") for h in range(2)]
+        third = keep.tile([P, S - NV], F32, name="third")
 
-        def entries(s):
-            return offsets[:, s * SL // 16:(s + 1) * SL // 16]
+        def entries(a, b):
+            return offsets[:, a // 16:b // 16]
 
-        def gather_in_place(j, s):
-            nc.vector.tensor_copy(grouped[s][:, :, j], planes[j][:].indirect(entries(s)))
+        def gather_in_place(j, a, b):
+            nc.vector.tensor_copy(grouped[:, a:b, j], planes[j][:].indirect(entries(a, b)))
 
-        def cast_gpsimd(a, b):
-            nc.gpsimd.tensor_scalar(last_bf[:, a:b], planes[3][:, a:b], 1.0, 0.0, MULT, ADD)
-
-        def cast_scalar(a, b):
-            nc.scalar.copy(last_bf[:, a:b], planes[3][:, a:b])
-
-        for s in (1, 2):
-            nc.vector.tensor_copy(third[s - 1][:], planes[2][:].indirect(entries(s)))
-            nc.scalar.copy(grouped[s][:, :, 2], third[s - 1][:])
-        gather_in_place(2, 0)
+        nc.vector.tensor_copy(third[:], planes[2][:].indirect(entries(NV, S)))
+        nc.scalar.copy(grouped[:, NV:S, 2], third[:])
+        gather_in_place(2, 0, NV)
         for j in (0, 1):
-            nc.vector.tensor_copy(pair[:, j, :], planes[j][:].indirect(entries(0)))
-            gather_in_place(j, 1)
-            gather_in_place(j, 2)
-        nc.scalar.copy(grouped[0][:, :, 0:2], pair[:].rearrange("p j s -> p s j"))
+            for h in range(2):
+                nc.vector.tensor_copy(pair[h][:, j, :], planes[j][:].indirect(entries(h * WOVEN // 2, (h + 1) * WOVEN // 2)))
+            gather_in_place(j, WOVEN, S)
+        for h in range(2):
+            nc.scalar.copy(grouped[:, h * WOVEN // 2:(h + 1) * WOVEN // 2, 0:2], pair[h][:].rearrange("p j s -> p s j"))
         for i in range(len(CHUNKS)):
-            cast_gpsimd(starts[i], starts[i] + GPSIMD_SHARE[i])
-            cast_scalar(starts[i] + GPSIMD_SHARE[i], starts[i + 1])
-        gather_in_place(3, 0)
-        for s in (1, 2):
-            nc.scalar.activation(grouped[s][:, :, 3], last_bf[:].indirect(entries(s)), COPY)
+            lo, mid, hi = starts[i], starts[i] + GPSIMD_SHARE[i], starts[i + 1] - VECTOR_SHARE[i]
+            if mid > lo:
+                nc.gpsimd.tensor_scalar(last_bf[:, lo:mid], planes[3][:, lo:mid], 1.0, 0.0, MULT, ADD)
+            if hi > mid:
+                nc.scalar.copy(last_bf[:, mid:hi], planes[3][:, mid:hi])
+            if starts[i + 1] > hi:
+                nc.vector.tensor_copy(last_bf[:, hi:starts[i + 1]], planes[3][:, hi:starts[i + 1]])
+        gather_in_place(3, 0, NV)
+        for a, b in ((640, 1536),):
+            nc.scalar.activation(grouped[:, a:b, 3], last_bf[:].indirect(entries(a, b)), COPY)
 
         w_grouped = keep.tile([P, N, PACK], BF16, name="w_grouped", align_bytes=64)
         w_codes = keep.tile([P, N], U32, name="w_codes", align_bytes=64)
         w_scales = keep.tile([P, N], U8, name="w_scales", align_bytes=64)
-        nc.gpsimd.tensor_scalar(w_grouped[:], w_raw[:].rearrange("p j m -> p m j"), 1.0, 0.0, MULT, ADD)
+        for m in range(MT):
+            nc.gpsimd.tensor_scalar(w_grouped[:, m * P:(m + 1) * P, :], w_raw[m][:].rearrange("p j m -> p m j"), 1.0, 0.0, MULT, ADD)
 
-        scales = [keep.tile([P, SL], U8, name=f"scales{s}", align_bytes=64) for s in range(3)]
-        codes = {}
+        scales = keep.tile([P, S], U8, name="scales", align_bytes=64)
+        early = keep.tile([P, 384], U32, name="early", tag="shared0", align_bytes=64)
+        EARLY = 384
 
-        def quant(s):
-            nc.vector.quantize_mx(out=codes[s].bitcast(FP8X4), scales=scales[s][:], in_=grouped[s][:].rearrange("p s j -> p (s j)"))
+        def codes(a, b):
+            return early[:, a:b] if a < EARLY else late[:, a - EARLY:b - EARLY]
 
-        def truth(d, m):
+        def quant(a, b):
+            nc.vector.quantize_mx(out=codes(a, b).bitcast(FP8X4), scales=scales[:, a:b], in_=grouped[:, a:b, :].rearrange("p s j -> p (s j)"))
+
+        def quant_w(a, b):
+            nc.vector.quantize_mx(out=w_codes[:, a:b].bitcast(FP8X4), scales=w_scales[:, a:b], in_=w_grouped[:, a:b, :].rearrange("p m j -> p (m j)"))
+
+        def product(d, m):
             bank = psum.tile([P, V], F32, name=f"bank{d}{m}")
-            lo, hi = d * V, (d + 1) * V
-            cut = lo + 2 * BLK if (lo + 2 * BLK - 1) // SL == lo // SL else lo + BLK
-            for a, b in ((lo, cut), (cut, hi)):
-                s, cols = a // SL, slice(a % SL, a % SL + b - a)
+            lo = d * V
+            for a, b in (((0, 256), (256, 384)), ((384, 640), (640, 768)), ((768, 1024), (1024, 1152)), ((1152, 1408), (1408, 1536)))[d]:
                 nc.tensor.matmul_mx(out=bank[:, a - lo:b - lo], lhsT=w_codes[:, m * P:(m + 1) * P].bitcast(FP8X4), lhsT_scale=w_scales[:, m * P:(m + 1) * P],
-                                    rhs=codes[s][:, cols].bitcast(FP8X4), rhs_scale=scales[s][:, cols], start=True, stop=True)
-            y = keep.tile([P, V], F32, name=f"truth{d}{m}")
-            nc.scalar.activation(y[:], bank[:], SIGMOID)
+                                    rhs=codes(a, b).bitcast(FP8X4), rhs_scale=scales[:, a:b], start=True, stop=True)
+            return bank
+
+        def truth(bank, name, a, b):
+            y = keep.tile([P, b - a], F32, name=name)
+            nc.scalar.activation(y[:], bank[:, a:b], SIGMOID)
             return y
 
-        codes0 = keep.tile([P, SL], U32, name="codes0", align_bytes=64)
-        codes[0] = codes0[:]
-        quant(0)
-        nc.vector.quantize_mx(out=w_codes[:].bitcast(FP8X4), scales=w_scales[:], in_=w_grouped[:].rearrange("p m j -> p (m j)"))
-        codes12 = keep.tile([P, 2 * SL], U32, name="codes12", tag="shared", align_bytes=64)
-        codes[1] = codes12[:, 0:SL]
-        codes[2] = codes12[:, SL:2 * SL]
-        quant(1)
-        quant(2)
+        quant_w(0, P)
+        for a, b in ((0, 256), (256, 384)):
+            quant(a, b)
+        quant_w(P, N)
+        late = keep.tile([P, S - EARLY], U32, name="late", tag="shared1", align_bytes=64)
+        for a, b in ((384, 640), (640, 768), (768, 1024), (1024, 1280), (1280, 1536)):
+            quant(a, b)
 
-        acc = [truth(0, m) for m in range(MT)]
+        acc = [truth(product(0, m), f"truth0{m}", 0, V) for m in range(MT)]
         for d in range(1, 4):
             for m in range(MT):
-                y = truth(d, m)
-                r = keep.tile([P, V], F32, name=f"prod{d}{m}")
-                nc.vector.tensor_tensor(r[:], acc[m][:], y[:], MULT)
-                acc[m] = r
-                if d == 3:
-                    nc.sync.dma_start(out=out[m * P:(m + 1) * P, :], in_=r[:])
+                bank = product(d, m)
+                for a, b in (((0, 256), (256, 384)) if (d, m) == (3, MT - 1) else ((0, V),)):
+                    y = truth(bank, f"truth{d}{m}_{a}", a, b)
+                    r = keep.tile([P, b - a], F32, name=f"prod{d}{m}_{a}")
+                    nc.vector.tensor_tensor(r[:], acc[m][:, a:b], y[:], MULT)
+                    if d == 3:
+                        nc.sync.dma_start(out=out[m * P:(m + 1) * P, a:b], in_=r[:])
+                if d < 3:
+                    acc[m] = r

@@ -18,15 +18,15 @@ ADD = mybir.AluOpType.add
 
 P = 128
 PACK = 4
-SL = 512
-BLK = 128
+PIECES = S // V
 MT = N // P
+PER_COLUMN = 16
+WIDE = 256
 
+ON_VECTOR = 640
+PAIRED = 512
 CHUNKS = (1344, 1152, 832, 512, 256)
-GPSIMD_SHARE = (960, 512, 352, 192, 0)
-VECTOR_SHARE = (0, 0, 0, 0, 0)
-NV = 640
-WOVEN = 512
+ON_GPSIMD = (960, 512, 352, 192, 0)
 
 
 def tile_picked_andpool_none_e_kernel(tc, xT, w1, offs, out):
@@ -35,7 +35,7 @@ def tile_picked_andpool_none_e_kernel(tc, xT, w1, offs, out):
         keep = ctx.enter_context(tc.tile_pool(name="keep", bufs=1))
         psum = ctx.enter_context(tc.psum_pool(name="psum", bufs=1))
 
-        offsets = keep.tile([P, S // 16], U16, name="offsets")
+        offsets = keep.tile([P, S // PER_COLUMN], U16, name="offsets")
         planes = [keep.tile([P, T], F32, name=f"plane{j}") for j in range(PACK)]
         last_bf = keep.tile([P, T], BF16, name="last_bf")
         w_raw = [keep.tile([P, PACK, P], F32, name=f"w_raw{m}", tag=f"shared{m}", align_bytes=64) for m in range(MT)]
@@ -44,48 +44,44 @@ def tile_picked_andpool_none_e_kernel(tc, xT, w1, offs, out):
         nc.sync.dma_start(offsets[:], offs)
         nc.sync.dma_start(out=planes[0][:], in_=x_rows[:, 0, :])
         nc.sync.dma_start(out=planes[1][:], in_=x_rows[:, 1, :])
-        starts = [sum(CHUNKS[:i]) for i in range(len(CHUNKS) + 1)]
-        for i in range(len(CHUNKS)):
-            nc.sync.dma_start(out=planes[3][:, starts[i]:starts[i + 1]], in_=x_rows[:, 3, starts[i]:starts[i + 1]])
+        edges = [sum(CHUNKS[:i]) for i in range(len(CHUNKS) + 1)]
+        for lo, hi in zip(edges, edges[1:]):
+            nc.sync.dma_start(out=planes[3][:, lo:hi], in_=x_rows[:, 3, lo:hi])
         w_rows = w1.rearrange("(p j) m -> p j m", j=PACK)
         for m in range(MT):
             nc.sync.dma_start(out=w_raw[m][:], in_=w_rows[:, :, m * P:(m + 1) * P])
 
-        warm_in = keep.tile([P, 1], F32, name="warm_in")
-        warm_out = keep.tile([P, 1], F32, name="warm_out")
-        nc.gpsimd.memset(warm_in[:], 0.0)
-        nc.scalar.activation(warm_out[:], warm_in[:], SIGMOID)
+        warm = keep.tile([P, 1], F32, name="warm")
+        nc.scalar.activation(warm[:], planes[2][:, 0:1], SIGMOID)
 
         grouped = keep.tile([P, S, PACK], BF16, name="grouped", align_bytes=64)
-        pair = [keep.tile([P, 2, WOVEN // 2], BF16, name=f"pair{h}") for h in range(2)]
-        third = keep.tile([P, S - NV], F32, name="third")
+        half = PAIRED // 2
+        pair = [keep.tile([P, 2, half], BF16, name=f"pair{h}") for h in range(2)]
+        staged2 = keep.tile([P, S - ON_VECTOR], F32, name="staged2")
 
         def entries(a, b):
-            return offsets[:, a // 16:b // 16]
+            return offsets[:, a // PER_COLUMN:b // PER_COLUMN]
 
-        def gather_in_place(j, a, b):
+        def gather_into_slot(j, a, b):
             nc.vector.tensor_copy(grouped[:, a:b, j], planes[j][:].indirect(entries(a, b)))
 
-        nc.vector.tensor_copy(third[:], planes[2][:].indirect(entries(NV, S)))
-        nc.scalar.copy(grouped[:, NV:S, 2], third[:])
-        gather_in_place(2, 0, NV)
+        nc.vector.tensor_copy(staged2[:], planes[2][:].indirect(entries(ON_VECTOR, S)))
+        nc.scalar.copy(grouped[:, ON_VECTOR:S, 2], staged2[:])
+        gather_into_slot(2, 0, ON_VECTOR)
+
         for j in (0, 1):
             for h in range(2):
-                nc.vector.tensor_copy(pair[h][:, j, :], planes[j][:].indirect(entries(h * WOVEN // 2, (h + 1) * WOVEN // 2)))
-            gather_in_place(j, WOVEN, S)
+                nc.vector.tensor_copy(pair[h][:, j, :], planes[j][:].indirect(entries(h * half, (h + 1) * half)))
+            gather_into_slot(j, PAIRED, S)
         for h in range(2):
-            nc.scalar.copy(grouped[:, h * WOVEN // 2:(h + 1) * WOVEN // 2, 0:2], pair[h][:].rearrange("p j s -> p s j"))
-        for i in range(len(CHUNKS)):
-            lo, mid, hi = starts[i], starts[i] + GPSIMD_SHARE[i], starts[i + 1] - VECTOR_SHARE[i]
-            if mid > lo:
-                nc.gpsimd.tensor_scalar(last_bf[:, lo:mid], planes[3][:, lo:mid], 1.0, 0.0, MULT, ADD)
-            if hi > mid:
-                nc.scalar.copy(last_bf[:, mid:hi], planes[3][:, mid:hi])
-            if starts[i + 1] > hi:
-                nc.vector.tensor_copy(last_bf[:, hi:starts[i + 1]], planes[3][:, hi:starts[i + 1]])
-        gather_in_place(3, 0, NV)
-        for a, b in ((640, 1536),):
-            nc.scalar.activation(grouped[:, a:b, 3], last_bf[:].indirect(entries(a, b)), COPY)
+            nc.scalar.copy(grouped[:, h * half:(h + 1) * half, 0:2], pair[h][:].rearrange("p j e -> p e j"))
+
+        for lo, hi, share in zip(edges, edges[1:], ON_GPSIMD):
+            if share:
+                nc.gpsimd.tensor_scalar(last_bf[:, lo:lo + share], planes[3][:, lo:lo + share], 1.0, 0.0, MULT, ADD)
+            nc.scalar.copy(last_bf[:, lo + share:hi], planes[3][:, lo + share:hi])
+        gather_into_slot(3, 0, ON_VECTOR)
+        nc.scalar.activation(grouped[:, ON_VECTOR:S, 3], last_bf[:].indirect(entries(ON_VECTOR, S)), COPY)
 
         w_grouped = keep.tile([P, N, PACK], BF16, name="w_grouped", align_bytes=64)
         w_codes = keep.tile([P, N], U32, name="w_codes", align_bytes=64)
@@ -94,24 +90,27 @@ def tile_picked_andpool_none_e_kernel(tc, xT, w1, offs, out):
             nc.gpsimd.tensor_scalar(w_grouped[:, m * P:(m + 1) * P, :], w_raw[m][:].rearrange("p j m -> p m j"), 1.0, 0.0, MULT, ADD)
 
         scales = keep.tile([P, S], U8, name="scales", align_bytes=64)
-        early = keep.tile([P, 384], U32, name="early", tag="shared0", align_bytes=64)
-        EARLY = 384
+        codes_first = keep.tile([P, V], U32, name="codes_first", tag="shared0", align_bytes=64)
 
         def codes(a, b):
-            return early[:, a:b] if a < EARLY else late[:, a - EARLY:b - EARLY]
+            return codes_first[:, a:b] if a < V else codes_rest[:, a - V:b - V]
 
-        def quant(a, b):
-            nc.vector.quantize_mx(out=codes(a, b).bitcast(FP8X4), scales=scales[:, a:b], in_=grouped[:, a:b, :].rearrange("p s j -> p (s j)"))
+        def quantise_entries(a, b):
+            nc.vector.quantize_mx(out=codes(a, b).bitcast(FP8X4), scales=scales[:, a:b],
+                                  in_=grouped[:, a:b, :].rearrange("p e j -> p (e j)"))
 
-        def quant_w(a, b):
-            nc.vector.quantize_mx(out=w_codes[:, a:b].bitcast(FP8X4), scales=w_scales[:, a:b], in_=w_grouped[:, a:b, :].rearrange("p m j -> p (m j)"))
+        def quantise_w(m):
+            cols = slice(m * P, (m + 1) * P)
+            nc.vector.quantize_mx(out=w_codes[:, cols].bitcast(FP8X4), scales=w_scales[:, cols],
+                                  in_=w_grouped[:, cols, :].rearrange("p m j -> p (m j)"))
 
-        def product(d, m):
+        def logits(d, m):
             bank = psum.tile([P, V], F32, name=f"bank{d}{m}")
-            lo = d * V
-            for a, b in (((0, 256), (256, 384)), ((384, 640), (640, 768)), ((768, 1024), (1024, 1152)), ((1152, 1408), (1408, 1536)))[d]:
-                nc.tensor.matmul_mx(out=bank[:, a - lo:b - lo], lhsT=w_codes[:, m * P:(m + 1) * P].bitcast(FP8X4), lhsT_scale=w_scales[:, m * P:(m + 1) * P],
-                                    rhs=codes(a, b).bitcast(FP8X4), rhs_scale=scales[:, a:b], start=True, stop=True)
+            cols = slice(m * P, (m + 1) * P)
+            for a, b in ((0, WIDE), (WIDE, V)):
+                nc.tensor.matmul_mx(out=bank[:, a:b], lhsT=w_codes[:, cols].bitcast(FP8X4), lhsT_scale=w_scales[:, cols],
+                                    rhs=codes(d * V + a, d * V + b).bitcast(FP8X4), rhs_scale=scales[:, d * V + a:d * V + b],
+                                    start=True, stop=True)
             return bank
 
         def truth(bank, name, a, b):
@@ -119,23 +118,26 @@ def tile_picked_andpool_none_e_kernel(tc, xT, w1, offs, out):
             nc.scalar.activation(y[:], bank[:, a:b], SIGMOID)
             return y
 
-        quant_w(0, P)
-        for a, b in ((0, 256), (256, 384)):
-            quant(a, b)
-        quant_w(P, N)
-        late = keep.tile([P, S - EARLY], U32, name="late", tag="shared1", align_bytes=64)
-        for a, b in ((384, 640), (640, 768), (768, 1024), (1024, 1280), (1280, 1536)):
-            quant(a, b)
+        quantise_w(0)
+        quantise_entries(0, WIDE)
+        quantise_entries(WIDE, V)
+        quantise_w(1)
+        codes_rest = keep.tile([P, S - V], U32, name="codes_rest", tag="shared1", align_bytes=64)
+        quantise_entries(V, V + WIDE)
+        quantise_entries(V + WIDE, 2 * V)
+        for a in range(2 * V, S, WIDE):
+            quantise_entries(a, a + WIDE)
 
-        acc = [truth(product(0, m), f"truth0{m}", 0, V) for m in range(MT)]
-        for d in range(1, 4):
+        running = [truth(logits(0, m), f"truth0{m}", 0, V) for m in range(MT)]
+        for d in range(1, PIECES):
             for m in range(MT):
-                bank = product(d, m)
-                for a, b in (((0, 256), (256, 384)) if (d, m) == (3, MT - 1) else ((0, V),)):
+                bank = logits(d, m)
+                very_last = (d, m) == (PIECES - 1, MT - 1)
+                for a, b in (((0, WIDE), (WIDE, V)) if very_last else ((0, V),)):
                     y = truth(bank, f"truth{d}{m}_{a}", a, b)
-                    r = keep.tile([P, b - a], F32, name=f"prod{d}{m}_{a}")
-                    nc.vector.tensor_tensor(r[:], acc[m][:, a:b], y[:], MULT)
-                    if d == 3:
-                        nc.sync.dma_start(out=out[m * P:(m + 1) * P, a:b], in_=r[:])
-                if d < 3:
-                    acc[m] = r
+                    product = keep.tile([P, b - a], F32, name=f"product{d}{m}_{a}")
+                    nc.vector.tensor_tensor(product[:], running[m][:, a:b], y[:], MULT)
+                    if d == PIECES - 1:
+                        nc.sync.dma_start(out=out[m * P:(m + 1) * P, a:b], in_=product[:])
+                    else:
+                        running[m] = product

@@ -25,8 +25,8 @@ WIDE = 256
 
 ON_VECTOR = 640
 PAIRED = 512
-CHUNKS = (1344, 1152, 832, 512, 256)
-ON_GPSIMD = (960, 512, 352, 192, 0)
+CHUNKS = (1280, 1344, 832, 448, 192)
+ON_GPSIMD = (960, 576, 320, 192, 0)
 
 
 def tile_picked_andpool_none_e_kernel(tc, xT, w1, offs, out):
@@ -104,19 +104,16 @@ def tile_picked_andpool_none_e_kernel(tc, xT, w1, offs, out):
             nc.vector.quantize_mx(out=w_codes[:, cols].bitcast(FP8X4), scales=w_scales[:, cols],
                                   in_=w_grouped[:, cols, :].rearrange("p m j -> p (m j)"))
 
-        def logits(d, m):
-            bank = psum.tile([P, V], F32, name=f"bank{d}{m}")
+        def multiply(bank, m, a, b):
             cols = slice(m * P, (m + 1) * P)
-            for a, b in ((0, WIDE), (WIDE, V)):
-                nc.tensor.matmul_mx(out=bank[:, a:b], lhsT=w_codes[:, cols].bitcast(FP8X4), lhsT_scale=w_scales[:, cols],
-                                    rhs=codes(d * V + a, d * V + b).bitcast(FP8X4), rhs_scale=scales[:, d * V + a:d * V + b],
-                                    start=True, stop=True)
-            return bank
+            nc.tensor.matmul_mx(out=bank, lhsT=w_codes[:, cols].bitcast(FP8X4), lhsT_scale=w_scales[:, cols],
+                                rhs=codes(a, b).bitcast(FP8X4), rhs_scale=scales[:, a:b], start=True, stop=True)
 
-        def truth(bank, name, a, b):
-            y = keep.tile([P, b - a], F32, name=name)
-            nc.scalar.activation(y[:], bank[:, a:b], SIGMOID)
-            return y
+        def logits(d, m, tag):
+            bank = psum.tile([P, V], F32, name=f"bank{d}{m}", tag=tag)
+            for a, b in ((0, WIDE), (WIDE, V)):
+                multiply(bank[:, a:b], m, d * V + a, d * V + b)
+            return bank
 
         quantise_w(0)
         quantise_entries(0, WIDE)
@@ -128,16 +125,31 @@ def tile_picked_andpool_none_e_kernel(tc, xT, w1, offs, out):
         for a in range(2 * V, S, WIDE):
             quantise_entries(a, a + WIDE)
 
-        running = [truth(logits(0, m), f"truth0{m}", 0, V) for m in range(MT)]
+        running = keep.tile([P, MT, V], F32, name="truth0")
+
+        def unit(view, bank, d, name):
+            y = keep.tile(list(bank.shape), F32, name=f"truth{d}{name}")
+            nc.scalar.activation(y[:], bank, SIGMOID)
+            nc.vector.tensor_tensor(view(product), view(running), y[:], MULT)
+
+        out_rows = out.rearrange("(m p) v -> p m v", p=P)
         for d in range(1, PIECES):
+            product = keep.tile([P, MT, V], F32, name=f"product{d}")
+            wide = psum.tile([P, MT, WIDE], F32, name=f"wide{d}")
+            rest = psum.tile([P, MT, V - WIDE], F32, name=f"rest{d}")
+            units = [(lambda t: t[:, 0, 0:WIDE], wide[:, 0, :]), (lambda t: t[:, 1, 0:WIDE], wide[:, 1, :]),
+                     (lambda t: t[:, :, WIDE:V], rest[:])]
+            if d == 1:
+                nc.scalar.activation(running[:, 0, :], logits(0, 0, "bank00")[:], SIGMOID)
+                second_bank = logits(0, 1, "bank01")
             for m in range(MT):
-                bank = logits(d, m)
-                very_last = (d, m) == (PIECES - 1, MT - 1)
-                for a, b in (((0, WIDE), (WIDE, V)) if very_last else ((0, V),)):
-                    y = truth(bank, f"truth{d}{m}_{a}", a, b)
-                    product = keep.tile([P, b - a], F32, name=f"product{d}{m}_{a}")
-                    nc.vector.tensor_tensor(product[:], running[m][:, a:b], y[:], MULT)
-                    if d == PIECES - 1:
-                        nc.sync.dma_start(out=out[m * P:(m + 1) * P, a:b], in_=product[:])
-                    else:
-                        running[m] = product
+                multiply(wide[:, m, :], m, d * V, d * V + WIDE)
+            for m in range(MT):
+                multiply(rest[:, m, :], m, d * V + WIDE, (d + 1) * V)
+            for u, (view, bank) in enumerate(units):
+                unit(view, bank, d, u)
+                if (d, u) == (1, 0):
+                    nc.scalar.activation(running[:, 1, :], second_bank[:], SIGMOID)
+                if d == PIECES - 1:
+                    nc.sync.dma_start(out=view(out_rows), in_=view(product))
+            running = product

@@ -22,6 +22,8 @@ PIECES = S // V
 MT = N // P
 PER_COLUMN = 16
 WIDE = 256
+REST = V - WIDE
+BANKS = 8
 
 ON_VECTOR = 640
 PAIRED = 512
@@ -109,15 +111,9 @@ def tile_picked_andpool_none_e_kernel(tc, xT, w1, offs, out):
             nc.tensor.matmul_mx(out=bank, lhsT=w_codes[:, cols].bitcast(FP8X4), lhsT_scale=w_scales[:, cols],
                                 rhs=codes(a, b).bitcast(FP8X4), rhs_scale=scales[:, a:b], start=True, stop=True)
 
-        def logits(d, m, tag):
-            bank = psum.tile([P, V], F32, name=f"bank{d}{m}", tag=tag)
-            for a, b in ((0, WIDE), (WIDE, V)):
-                multiply(bank[:, a:b], m, d * V + a, d * V + b)
-            return bank
-
         quantise_w(0)
-        quantise_entries(0, WIDE)
-        quantise_entries(WIDE, V)
+        quantise_entries(0, REST)
+        quantise_entries(REST, V)
         quantise_w(1)
         codes_rest = keep.tile([P, S - V], U32, name="codes_rest", tag="shared1", align_bytes=64)
         quantise_entries(V, V + WIDE)
@@ -125,31 +121,27 @@ def tile_picked_andpool_none_e_kernel(tc, xT, w1, offs, out):
         for a in range(2 * V, S, WIDE):
             quantise_entries(a, a + WIDE)
 
-        running = keep.tile([P, MT, V], F32, name="truth0")
+        def sigmoid_unit(y, parts):
+            bank = psum.tile([P, sum(b - a for m, a, b in parts)], F32, name="bank", bufs=BANKS)
+            at = 0
+            for m, a, b in parts:
+                multiply(bank[:, at:at + b - a], m, a, b)
+                at = at + b - a
+            nc.scalar.activation(y, bank[:], SIGMOID)
 
-        def unit(view, bank, d, name):
-            y = keep.tile(list(bank.shape), F32, name=f"truth{d}{name}")
-            nc.scalar.activation(y[:], bank, SIGMOID)
-            nc.vector.tensor_tensor(view(product), view(running), y[:], MULT)
+        running = keep.tile([P, MT, V], F32, name="truth0")
+        sigmoid_unit(running[:, 0, 0:REST], [(0, 0, REST)])
+        sigmoid_unit(running[:, 0, REST:V], [(0, REST, V)])
+        sigmoid_unit(running[:, 1, :], [(1, 0, REST), (1, REST, V)])
 
         out_rows = out.rearrange("(m p) v -> p m v", p=P)
         for d in range(1, PIECES):
             product = keep.tile([P, MT, V], F32, name=f"product{d}")
-            wide = psum.tile([P, MT, WIDE], F32, name=f"wide{d}")
-            rest = psum.tile([P, MT, V - WIDE], F32, name=f"rest{d}")
-            units = [(lambda t: t[:, 0, 0:WIDE], wide[:, 0, :]), (lambda t: t[:, 1, 0:WIDE], wide[:, 1, :]),
-                     (lambda t: t[:, :, WIDE:V], rest[:])]
-            if d == 1:
-                nc.scalar.activation(running[:, 0, :], logits(0, 0, "bank00")[:], SIGMOID)
-                second_bank = logits(0, 1, "bank01")
-            for m in range(MT):
-                multiply(wide[:, m, :], m, d * V, d * V + WIDE)
-            for m in range(MT):
-                multiply(rest[:, m, :], m, d * V + WIDE, (d + 1) * V)
-            for u, (view, bank) in enumerate(units):
-                unit(view, bank, d, u)
-                if (d, u) == (1, 0):
-                    nc.scalar.activation(running[:, 1, :], second_bank[:], SIGMOID)
+            for tiles, a, b in (((0,), 0, WIDE), ((1,), 0, WIDE), ((0, 1), WIDE, V)):
+                rows = slice(tiles[0], tiles[-1] + 1)
+                y = keep.tile([P, len(tiles), b - a], F32, name=f"truth{d}_{tiles[-1]}_{a}")
+                sigmoid_unit(y[:].rearrange("p m v -> p (m v)"), [(m, d * V + a, d * V + b) for m in tiles])
+                nc.vector.tensor_tensor(product[:, rows, a:b], running[:, rows, a:b], y[:], MULT)
                 if d == PIECES - 1:
-                    nc.sync.dma_start(out=view(out_rows), in_=view(product))
+                    nc.sync.dma_start(out=out_rows[:, rows, a:b], in_=product[:, rows, a:b])
             running = product

@@ -7,6 +7,7 @@ FLOPS = 2 * K * S * N
 
 F32 = mybir.dt.float32
 BF16 = mybir.dt.bfloat16
+I32 = mybir.dt.int32
 U32 = mybir.dt.uint32
 U16 = mybir.dt.uint16
 U8 = mybir.dt.uint8
@@ -24,11 +25,12 @@ PER_COLUMN = 16
 WIDE = 256
 REST = V - WIDE
 BANKS = 8
-
 ON_VECTOR = 640
-PAIRED = 512
-CHUNKS = (1280, 1344, 832, 448, 192)
-ON_GPSIMD = (960, 576, 320, 192, 0)
+WOVEN_BY_SCALAR = ((640, 768), (768, 1024))
+WOVEN_BY_VECTOR = ((1024, 1536),)
+CHUNKS = (1792, 1408, 704, 192)
+ON_GPSIMD = (896, 384, 0, 0)
+ROUNDED_BY_VECTOR = (0, 256, 448, 0)
 
 
 def tile_picked_andpool_none_e_kernel(tc, xT, w1, offs, out):
@@ -38,8 +40,7 @@ def tile_picked_andpool_none_e_kernel(tc, xT, w1, offs, out):
         psum = ctx.enter_context(tc.psum_pool(name="psum", bufs=1))
 
         offsets = keep.tile([P, S // PER_COLUMN], U16, name="offsets")
-        planes = [keep.tile([P, T], F32, name=f"plane{j}") for j in range(PACK)]
-        last_bf = keep.tile([P, T], BF16, name="last_bf")
+        planes = [keep.tile([P, T], F32, name=f"plane{j}", tag=f"plane{j}") for j in range(PACK)]
         w_raw = [keep.tile([P, PACK, P], F32, name=f"w_raw{m}", tag=f"shared{m}", align_bytes=64) for m in range(MT)]
         x_rows = xT.rearrange("(p j) t -> p j t", j=PACK)
         nc.sync.dma_start(out=planes[2][:], in_=x_rows[:, 2, :])
@@ -56,34 +57,24 @@ def tile_picked_andpool_none_e_kernel(tc, xT, w1, offs, out):
         warm = keep.tile([P, 1], F32, name="warm")
         nc.scalar.activation(warm[:], planes[2][:, 0:1], SIGMOID)
 
-        grouped = keep.tile([P, S, PACK], BF16, name="grouped", align_bytes=64)
-        half = PAIRED // 2
-        pair = [keep.tile([P, 2, half], BF16, name=f"pair{h}") for h in range(2)]
-        staged2 = keep.tile([P, S - ON_VECTOR], F32, name="staged2")
-
         def entries(a, b):
             return offsets[:, a // PER_COLUMN:b // PER_COLUMN]
 
-        def gather_into_slot(j, a, b):
-            nc.vector.tensor_copy(grouped[:, a:b, j], planes[j][:].indirect(entries(a, b)))
+        direct = keep.tile([P, ON_VECTOR, PACK], BF16, name="direct", tag="direct", align_bytes=64)
+        pairs = keep.tile([P, 2, S - ON_VECTOR, 2], BF16, name="pairs")
+        for j in (2, 0, 1):
+            nc.vector.tensor_copy(pairs[:, j // 2, :, j % 2], planes[j][:].indirect(entries(ON_VECTOR, S)))
+            nc.vector.tensor_copy(direct[:, :, j], planes[j][:].indirect(entries(0, ON_VECTOR)))
 
-        nc.vector.tensor_copy(staged2[:], planes[2][:].indirect(entries(ON_VECTOR, S)))
-        nc.scalar.copy(grouped[:, ON_VECTOR:S, 2], staged2[:])
-        gather_into_slot(2, 0, ON_VECTOR)
-
-        for j in (0, 1):
-            for h in range(2):
-                nc.vector.tensor_copy(pair[h][:, j, :], planes[j][:].indirect(entries(h * half, (h + 1) * half)))
-            gather_into_slot(j, PAIRED, S)
-        for h in range(2):
-            nc.scalar.copy(grouped[:, h * half:(h + 1) * half, 0:2], pair[h][:].rearrange("p j e -> p e j"))
-
-        for lo, hi, share in zip(edges, edges[1:], ON_GPSIMD):
+        last_bf = keep.tile([P, T], BF16, name="last_bf", tag="plane2")
+        for lo, hi, share, tail in zip(edges, edges[1:], ON_GPSIMD, ROUNDED_BY_VECTOR):
             if share:
                 nc.gpsimd.tensor_scalar(last_bf[:, lo:lo + share], planes[3][:, lo:lo + share], 1.0, 0.0, MULT, ADD)
-            nc.scalar.copy(last_bf[:, lo + share:hi], planes[3][:, lo + share:hi])
-        gather_into_slot(3, 0, ON_VECTOR)
-        nc.scalar.activation(grouped[:, ON_VECTOR:S, 3], last_bf[:].indirect(entries(ON_VECTOR, S)), COPY)
+            nc.scalar.copy(last_bf[:, lo + share:hi - tail], planes[3][:, lo + share:hi - tail])
+            if tail:
+                nc.vector.tensor_copy(last_bf[:, hi - tail:hi], planes[3][:, hi - tail:hi])
+        nc.vector.tensor_copy(direct[:, :, 3], planes[3][:].indirect(entries(0, ON_VECTOR)))
+        nc.scalar.activation(pairs[:, 1, :, 1], last_bf[:].indirect(entries(ON_VECTOR, S)), COPY)
 
         w_grouped = keep.tile([P, N, PACK], BF16, name="w_grouped", align_bytes=64)
         w_codes = keep.tile([P, N], U32, name="w_codes", align_bytes=64)
@@ -93,33 +84,49 @@ def tile_picked_andpool_none_e_kernel(tc, xT, w1, offs, out):
 
         scales = keep.tile([P, S], U8, name="scales", align_bytes=64)
         codes_first = keep.tile([P, V], U32, name="codes_first", tag="shared0", align_bytes=64)
+        grouped = {}
+
+        def weave(a, b):
+            words = pairs[:].rearrange("p r e h -> p r (e h)")
+            grouped[a] = keep.tile([P, (b - a) * PACK], BF16, name=f"grouped{a}", tag=f"grouped{a}" if (a, b) in WOVEN_BY_SCALAR else "direct", align_bytes=64)
+            copy, dtype = (nc.scalar.copy, U32) if (a, b) in WOVEN_BY_SCALAR else (nc.vector.tensor_copy, I32)
+            copy(grouped[a][:].bitcast(dtype).rearrange("p (e r) -> p e r", r=2),
+                 words.bitcast(dtype)[:, :, a - ON_VECTOR:b - ON_VECTOR].rearrange("p r e -> p e r"))
+
+        def woven(a, b):
+            start = max(s for s in grouped if s <= a)
+            return grouped[start][:, (a - start) * PACK:(b - start) * PACK]
 
         def codes(a, b):
             return codes_first[:, a:b] if a < V else codes_rest[:, a - V:b - V]
 
         def quantise_entries(a, b):
             nc.vector.quantize_mx(out=codes(a, b).bitcast(FP8X4), scales=scales[:, a:b],
-                                  in_=grouped[:, a:b, :].rearrange("p e j -> p (e j)"))
+                                  in_=direct[:, a:b, :].rearrange("p e j -> p (e j)") if a < ON_VECTOR else woven(a, b))
 
         def quantise_w(m):
             cols = slice(m * P, (m + 1) * P)
             nc.vector.quantize_mx(out=w_codes[:, cols].bitcast(FP8X4), scales=w_scales[:, cols],
                                   in_=w_grouped[:, cols, :].rearrange("p m j -> p (m j)"))
 
-        def multiply(bank, m, a, b):
-            cols = slice(m * P, (m + 1) * P)
-            nc.tensor.matmul_mx(out=bank, lhsT=w_codes[:, cols].bitcast(FP8X4), lhsT_scale=w_scales[:, cols],
-                                rhs=codes(a, b).bitcast(FP8X4), rhs_scale=scales[:, a:b], start=True, stop=True)
-
         quantise_w(0)
         quantise_entries(0, REST)
         quantise_entries(REST, V)
         quantise_w(1)
         codes_rest = keep.tile([P, S - V], U32, name="codes_rest", tag="shared1", align_bytes=64)
-        quantise_entries(V, V + WIDE)
-        quantise_entries(V + WIDE, 2 * V)
-        for a in range(2 * V, S, WIDE):
-            quantise_entries(a, a + WIDE)
+        quantise_entries(V, ON_VECTOR)
+        for a, b in WOVEN_BY_SCALAR:
+            weave(a, b)
+        weave(*WOVEN_BY_VECTOR[0])
+        quantise_entries(*WOVEN_BY_SCALAR[0])
+        quantise_entries(1024, 1280)
+        quantise_entries(*WOVEN_BY_SCALAR[1])
+        quantise_entries(1280, 1536)
+
+        def multiply(bank, m, a, b):
+            cols = slice(m * P, (m + 1) * P)
+            nc.tensor.matmul_mx(out=bank, lhsT=w_codes[:, cols].bitcast(FP8X4), lhsT_scale=w_scales[:, cols],
+                                rhs=codes(a, b).bitcast(FP8X4), rhs_scale=scales[:, a:b], start=True, stop=True)
 
         def sigmoid_unit(y, parts):
             bank = psum.tile([P, sum(b - a for m, a, b in parts)], F32, name="bank", bufs=BANKS)
@@ -133,7 +140,6 @@ def tile_picked_andpool_none_e_kernel(tc, xT, w1, offs, out):
         sigmoid_unit(running[:, 0, 0:REST], [(0, 0, REST)])
         sigmoid_unit(running[:, 0, REST:V], [(0, REST, V)])
         sigmoid_unit(running[:, 1, :], [(1, 0, REST), (1, REST, V)])
-
         out_rows = out.rearrange("(m p) v -> p m v", p=P)
         for d in range(1, PIECES):
             product = keep.tile([P, MT, V], F32, name=f"product{d}")

@@ -29,7 +29,7 @@ ON_VECTOR = 640
 WOVEN_BY_SCALAR = ((640, 768), (768, 1024))
 WOVEN_BY_VECTOR = ((1024, 1536),)
 CHUNKS = (1792, 1408, 704, 192)
-ON_GPSIMD = (896, 384, 0, 0)
+ON_GPSIMD = (896, 448, 0, 0)
 ROUNDED_BY_VECTOR = (0, 256, 448, 0)
 
 
@@ -117,11 +117,10 @@ def tile_picked_andpool_none_e_kernel(tc, xT, w1, offs, out):
         quantise_entries(V, ON_VECTOR)
         for a, b in WOVEN_BY_SCALAR:
             weave(a, b)
-        weave(*WOVEN_BY_VECTOR[0])
         quantise_entries(*WOVEN_BY_SCALAR[0])
-        quantise_entries(1024, 1280)
-        quantise_entries(*WOVEN_BY_SCALAR[1])
-        quantise_entries(1280, 1536)
+        weave(*WOVEN_BY_VECTOR[0])
+        for a in range(2 * V, S, WIDE):
+            quantise_entries(a, a + WIDE)
 
         def multiply(bank, m, a, b):
             cols = slice(m * P, (m + 1) * P)

@@ -7,7 +7,6 @@ FLOPS = 2 * K * S * N
 
 F32 = mybir.dt.float32
 BF16 = mybir.dt.bfloat16
-I32 = mybir.dt.int32
 U32 = mybir.dt.uint32
 U16 = mybir.dt.uint16
 U8 = mybir.dt.uint8
@@ -22,59 +21,54 @@ PACK = 4
 PIECES = S // V
 MT = N // P
 PER_COLUMN = 16
-WIDE = 256
-REST = V - WIDE
 BANKS = 8
-ON_VECTOR = 640
-WOVEN_BY_SCALAR = ((640, 768), (768, 1024))
-WOVEN_BY_VECTOR = ((1024, 1536),)
-CHUNKS = (1792, 1408, 704, 192)
-ON_GPSIMD = (896, 448, 0, 0)
-ROUNDED_BY_VECTOR = (0, 256, 448, 0)
+FIRST = 128
+DIRECT = 768
+HANDED = 256
+SCALAR_CUT = 1280
 
 
 def tile_picked_andpool_none_e_kernel(tc, xT, w1, offs, out):
     nc = tc.nc
     with ExitStack() as ctx:
         keep = ctx.enter_context(tc.tile_pool(name="keep", bufs=1))
+        reuse = ctx.enter_context(tc.tile_pool(name="reuse", bufs=1))
         psum = ctx.enter_context(tc.psum_pool(name="psum", bufs=1))
 
         offsets = keep.tile([P, S // PER_COLUMN], U16, name="offsets")
-        planes = [keep.tile([P, T], F32, name=f"plane{j}", tag=f"plane{j}") for j in range(PACK)]
-        w_raw = [keep.tile([P, PACK, P], F32, name=f"w_raw{m}", tag=f"shared{m}", align_bytes=64) for m in range(MT)]
+        planes = [keep.tile([P, T], F32, name=f"plane{j}") for j in range(PACK)]
+        w_raw = [reuse.tile([P, PACK, P], F32, name="w_raw0", align_bytes=64, offset=0), keep.tile([P, PACK, P], F32, name="w_raw1")]
         x_rows = xT.rearrange("(p j) t -> p j t", j=PACK)
-        nc.sync.dma_start(out=planes[2][:], in_=x_rows[:, 2, :])
-        nc.sync.dma_start(offsets[:], offs)
         nc.sync.dma_start(out=planes[0][:], in_=x_rows[:, 0, :])
-        nc.sync.dma_start(out=planes[1][:], in_=x_rows[:, 1, :])
-        edges = [sum(CHUNKS[:i]) for i in range(len(CHUNKS) + 1)]
-        for lo, hi in zip(edges, edges[1:]):
-            nc.sync.dma_start(out=planes[3][:, lo:hi], in_=x_rows[:, 3, lo:hi])
+        nc.sync.dma_start(offsets[:], offs)
+        for j in range(1, PACK):
+            nc.sync.dma_start(out=planes[j][:], in_=x_rows[:, j, :])
         w_rows = w1.rearrange("(p j) m -> p j m", j=PACK)
         for m in range(MT):
             nc.sync.dma_start(out=w_raw[m][:], in_=w_rows[:, :, m * P:(m + 1) * P])
 
         warm = keep.tile([P, 1], F32, name="warm")
-        nc.scalar.activation(warm[:], planes[2][:, 0:1], SIGMOID)
+        nc.scalar.activation(warm[:], planes[0][:, 0:1], SIGMOID)
 
         def entries(a, b):
             return offsets[:, a // PER_COLUMN:b // PER_COLUMN]
 
-        direct = keep.tile([P, ON_VECTOR, PACK], BF16, name="direct", tag="direct", align_bytes=64)
-        pairs = keep.tile([P, 2, S - ON_VECTOR, 2], BF16, name="pairs")
-        for j in (2, 0, 1):
-            nc.vector.tensor_copy(pairs[:, j // 2, :, j % 2], planes[j][:].indirect(entries(ON_VECTOR, S)))
-            nc.vector.tensor_copy(direct[:, :, j], planes[j][:].indirect(entries(0, ON_VECTOR)))
+        grouped = keep.tile([P, S, PACK], BF16, name="grouped", align_bytes=64)
+        border = DIRECT + HANDED
+        for j in range(PACK - 1):
+            nc.vector.tensor_copy(grouped[:, :border, j], planes[j][:].indirect(entries(0, border)))
+            flat = keep.tile([P, S - border], BF16, name=f"flat{j}")
+            nc.scalar.activation(flat[:], planes[j][:].indirect(entries(border, S)), COPY)
+            nc.scalar.copy(grouped[:, border:, j], flat[:])
 
-        last_bf = keep.tile([P, T], BF16, name="last_bf", tag="plane2")
-        for lo, hi, share, tail in zip(edges, edges[1:], ON_GPSIMD, ROUNDED_BY_VECTOR):
-            if share:
-                nc.gpsimd.tensor_scalar(last_bf[:, lo:lo + share], planes[3][:, lo:lo + share], 1.0, 0.0, MULT, ADD)
-            nc.scalar.copy(last_bf[:, lo + share:hi - tail], planes[3][:, lo + share:hi - tail])
-            if tail:
-                nc.vector.tensor_copy(last_bf[:, hi - tail:hi], planes[3][:, hi - tail:hi])
-        nc.vector.tensor_copy(direct[:, :, 3], planes[3][:].indirect(entries(0, ON_VECTOR)))
-        nc.scalar.activation(pairs[:, 1, :, 1], last_bf[:].indirect(entries(ON_VECTOR, S)), COPY)
+        last = PACK - 1
+        nc.vector.tensor_copy(grouped[:, :DIRECT, last], planes[last][:].indirect(entries(0, DIRECT)))
+        spans = ((SCALAR_CUT, S), (border, SCALAR_CUT))
+        flats = [keep.tile([P, b - a], BF16, name=f"last{a}") for a, b in spans]
+        for (a, b), flat in zip(spans, flats):
+            nc.scalar.activation(flat[:], planes[last][:].indirect(entries(a, b)), COPY)
+        for (a, b), flat in zip(spans, flats):
+            nc.scalar.copy(grouped[:, a:b, last], flat[:])
 
         w_grouped = keep.tile([P, N, PACK], BF16, name="w_grouped", align_bytes=64)
         w_codes = keep.tile([P, N], U32, name="w_codes", align_bytes=64)
@@ -82,27 +76,13 @@ def tile_picked_andpool_none_e_kernel(tc, xT, w1, offs, out):
         for m in range(MT):
             nc.gpsimd.tensor_scalar(w_grouped[:, m * P:(m + 1) * P, :], w_raw[m][:].rearrange("p j m -> p m j"), 1.0, 0.0, MULT, ADD)
 
+        handed = reuse.tile([P, HANDED], BF16, name="handed", align_bytes=64, offset=0)
+        nc.scalar.activation(handed[:], planes[last][:].indirect(entries(DIRECT, border)), COPY)
         scales = keep.tile([P, S], U8, name="scales", align_bytes=64)
-        codes_first = keep.tile([P, V], U32, name="codes_first", tag="shared0", align_bytes=64)
-        grouped = {}
-
-        def weave(a, b):
-            words = pairs[:].rearrange("p r e h -> p r (e h)")
-            grouped[a] = keep.tile([P, (b - a) * PACK], BF16, name=f"grouped{a}", tag=f"grouped{a}" if (a, b) in WOVEN_BY_SCALAR else "direct", align_bytes=64)
-            copy, dtype = (nc.scalar.copy, U32) if (a, b) in WOVEN_BY_SCALAR else (nc.vector.tensor_copy, I32)
-            copy(grouped[a][:].bitcast(dtype).rearrange("p (e r) -> p e r", r=2),
-                 words.bitcast(dtype)[:, :, a - ON_VECTOR:b - ON_VECTOR].rearrange("p r e -> p e r"))
-
-        def woven(a, b):
-            start = max(s for s in grouped if s <= a)
-            return grouped[start][:, (a - start) * PACK:(b - start) * PACK]
-
-        def codes(a, b):
-            return codes_first[:, a:b] if a < V else codes_rest[:, a - V:b - V]
+        codes = reuse.tile([P, S], U32, name="codes", align_bytes=64, offset=512)
 
         def quantise_entries(a, b):
-            nc.vector.quantize_mx(out=codes(a, b).bitcast(FP8X4), scales=scales[:, a:b],
-                                  in_=direct[:, a:b, :].rearrange("p e j -> p (e j)") if a < ON_VECTOR else woven(a, b))
+            nc.vector.quantize_mx(out=codes[:, a:b].bitcast(FP8X4), scales=scales[:, a:b], in_=grouped[:, a:b, :].rearrange("p e j -> p (e j)"))
 
         def quantise_w(m):
             cols = slice(m * P, (m + 1) * P)
@@ -110,43 +90,43 @@ def tile_picked_andpool_none_e_kernel(tc, xT, w1, offs, out):
                                   in_=w_grouped[:, cols, :].rearrange("p m j -> p (m j)"))
 
         quantise_w(0)
-        quantise_entries(0, REST)
-        quantise_entries(REST, V)
+        quantise_entries(0, FIRST)
+        quantise_entries(FIRST, V)
         quantise_w(1)
-        codes_rest = keep.tile([P, S - V], U32, name="codes_rest", tag="shared1", align_bytes=64)
-        quantise_entries(V, ON_VECTOR)
-        for a, b in WOVEN_BY_SCALAR:
-            weave(a, b)
-        quantise_entries(*WOVEN_BY_SCALAR[0])
-        weave(*WOVEN_BY_VECTOR[0])
-        for a in range(2 * V, S, WIDE):
-            quantise_entries(a, a + WIDE)
+        quantise_entries(V, 2 * V)
+        quantise_entries(3 * V, S)
+        nc.vector.tensor_copy(grouped[:, DIRECT:border, last], handed[:])
+        quantise_entries(border, 3 * V)
+        quantise_entries(2 * V, border)
 
-        def multiply(bank, m, a, b):
-            cols = slice(m * P, (m + 1) * P)
-            nc.tensor.matmul_mx(out=bank, lhsT=w_codes[:, cols].bitcast(FP8X4), lhsT_scale=w_scales[:, cols],
-                                rhs=codes(a, b).bitcast(FP8X4), rhs_scale=scales[:, a:b], start=True, stop=True)
+        truth = keep.tile([P, MT, S], F32, name="truth")
 
-        def sigmoid_unit(y, parts):
-            bank = psum.tile([P, sum(b - a for m, a, b in parts)], F32, name="bank", bufs=BANKS)
-            at = 0
-            for m, a, b in parts:
-                multiply(bank[:, at:at + b - a], m, a, b)
-                at = at + b - a
-            nc.scalar.activation(y, bank[:], SIGMOID)
+        def sigmoid_unit(tiles, a, b, cuts=()):
+            bank = psum.tile([P, len(tiles), b - a], F32, name="bank", bufs=BANKS)
+            edges = [a, *cuts, b]
+            for i, m in enumerate(tiles):
+                cols = slice(m * P, (m + 1) * P)
+                for lo, hi in zip(edges, edges[1:]):
+                    nc.tensor.matmul_mx(out=bank[:, i, lo - a:hi - a], lhsT=w_codes[:, cols].bitcast(FP8X4), lhsT_scale=w_scales[:, cols],
+                                        rhs=codes[:, lo:hi].bitcast(FP8X4), rhs_scale=scales[:, lo:hi], start=True, stop=True)
+            nc.scalar.activation(truth[:, tiles[0]:tiles[-1] + 1, a:b], bank[:], SIGMOID)
 
-        running = keep.tile([P, MT, V], F32, name="truth0")
-        sigmoid_unit(running[:, 0, 0:REST], [(0, 0, REST)])
-        sigmoid_unit(running[:, 0, REST:V], [(0, REST, V)])
-        sigmoid_unit(running[:, 1, :], [(1, 0, REST), (1, REST, V)])
         out_rows = out.rearrange("(m p) v -> p m v", p=P)
-        for d in range(1, PIECES):
-            product = keep.tile([P, MT, V], F32, name=f"product{d}")
-            for tiles, a, b in (((0,), 0, WIDE), ((1,), 0, WIDE), ((0, 1), WIDE, V)):
-                rows = slice(tiles[0], tiles[-1] + 1)
-                y = keep.tile([P, len(tiles), b - a], F32, name=f"truth{d}_{tiles[-1]}_{a}")
-                sigmoid_unit(y[:].rearrange("p m v -> p (m v)"), [(m, d * V + a, d * V + b) for m in tiles])
-                nc.vector.tensor_tensor(product[:, rows, a:b], running[:, rows, a:b], y[:], MULT)
-                if d == PIECES - 1:
-                    nc.sync.dma_start(out=out_rows[:, rows, a:b], in_=product[:, rows, a:b])
-            running = product
+        two = keep.tile([P, MT, V], F32, name="two")
+        three = keep.tile([P, MT, V], F32, name="three")
+        four = keep.tile([P, MT, V], F32, name="four")
+
+        def multiply(product, running, d, tiles, a, b):
+            rows = slice(tiles[0], tiles[-1] + 1)
+            nc.vector.tensor_tensor(product[:, rows, a:b], running[:, rows, a:b], truth[:, rows, d * V + a:d * V + b], MULT)
+
+        sigmoid_unit((0,), 0, FIRST)
+        sigmoid_unit((0,), FIRST, V)
+        sigmoid_unit((1,), 0, V, (FIRST,))
+        for product, running, d in ((two, truth, 1), (three, two, 3), (four, three, 2)):
+            for tiles, a, b in (((0,), 0, 256), ((1,), 0, 256), ((0, 1), 256, V)):
+                sigmoid_unit(tiles, d * V + a, d * V + b)
+                multiply(product, running, d, tiles, a, b)
+                if product is four:
+                    rows = slice(tiles[0], tiles[-1] + 1)
+                    nc.sync.dma_start(out=out_rows[:, rows, a:b], in_=four[:, rows, a:b])

@@ -23,8 +23,8 @@ MT = N // P
 PER_COLUMN = 16
 BANKS = 8
 FIRST = 128
-DIRECT = 768
-HANDED = 256
+DIRECT = 640
+HANDED = 448
 SCALAR_CUT = 1280
 
 
@@ -37,7 +37,7 @@ def tile_picked_andpool_none_e_kernel(tc, xT, w1, offs, out):
 
         offsets = keep.tile([P, S // PER_COLUMN], U16, name="offsets")
         planes = [keep.tile([P, T], F32, name=f"plane{j}") for j in range(PACK)]
-        w_raw = [reuse.tile([P, PACK, P], F32, name="w_raw0", align_bytes=64, offset=0), keep.tile([P, PACK, P], F32, name="w_raw1")]
+        w_raw = [reuse.tile([P, PACK, P], F32, name="w_raw0", align_bytes=64, offset=0), keep.tile([P, PACK, P], F32, name="w_raw1", tag="second", align_bytes=64)]
         x_rows = xT.rearrange("(p j) t -> p j t", j=PACK)
         nc.sync.dma_start(out=planes[0][:], in_=x_rows[:, 0, :])
         nc.sync.dma_start(offsets[:], offs)
@@ -79,10 +79,14 @@ def tile_picked_andpool_none_e_kernel(tc, xT, w1, offs, out):
         handed = reuse.tile([P, HANDED], BF16, name="handed", align_bytes=64, offset=0)
         nc.scalar.activation(handed[:], planes[last][:].indirect(entries(DIRECT, border)), COPY)
         scales = keep.tile([P, S], U8, name="scales", align_bytes=64)
-        codes = reuse.tile([P, S], U32, name="codes", align_bytes=64, offset=512)
+        codes_first = reuse.tile([P, DIRECT], U32, name="codes_first", align_bytes=64, offset=896)
+        codes_rest = keep.tile([P, S - DIRECT], U32, name="codes_rest", tag="second", align_bytes=64)
+
+        def codes(a, b):
+            return codes_first[:, a:b] if a < DIRECT else codes_rest[:, a - DIRECT:b - DIRECT]
 
         def quantise_entries(a, b):
-            nc.vector.quantize_mx(out=codes[:, a:b].bitcast(FP8X4), scales=scales[:, a:b], in_=grouped[:, a:b, :].rearrange("p e j -> p (e j)"))
+            nc.vector.quantize_mx(out=codes(a, b).bitcast(FP8X4), scales=scales[:, a:b], in_=grouped[:, a:b, :].rearrange("p e j -> p (e j)"))
 
         def quantise_w(m):
             cols = slice(m * P, (m + 1) * P)
@@ -92,12 +96,13 @@ def tile_picked_andpool_none_e_kernel(tc, xT, w1, offs, out):
         quantise_w(0)
         quantise_entries(0, FIRST)
         quantise_entries(FIRST, V)
+        quantise_entries(V, DIRECT)
         quantise_w(1)
-        quantise_entries(V, 2 * V)
         quantise_entries(3 * V, S)
-        nc.vector.tensor_copy(grouped[:, DIRECT:border, last], handed[:])
-        quantise_entries(border, 3 * V)
-        quantise_entries(2 * V, border)
+        nc.vector.tensor_copy(grouped[:, DIRECT:DIRECT + 256, last], handed[:, :256])
+        nc.vector.tensor_copy(grouped[:, DIRECT + 256:border, last], handed[:, 256:])
+        quantise_entries(DIRECT, DIRECT + 256)
+        quantise_entries(DIRECT + 256, 3 * V)
 
         truth = keep.tile([P, MT, S], F32, name="truth")
 
@@ -108,7 +113,7 @@ def tile_picked_andpool_none_e_kernel(tc, xT, w1, offs, out):
                 cols = slice(m * P, (m + 1) * P)
                 for lo, hi in zip(edges, edges[1:]):
                     nc.tensor.matmul_mx(out=bank[:, i, lo - a:hi - a], lhsT=w_codes[:, cols].bitcast(FP8X4), lhsT_scale=w_scales[:, cols],
-                                        rhs=codes[:, lo:hi].bitcast(FP8X4), rhs_scale=scales[:, lo:hi], start=True, stop=True)
+                                        rhs=codes(lo, hi).bitcast(FP8X4), rhs_scale=scales[:, lo:hi], start=True, stop=True)
             nc.scalar.activation(truth[:, tiles[0]:tiles[-1] + 1, a:b], bank[:], SIGMOID)
 
         out_rows = out.rearrange("(m p) v -> p m v", p=P)
@@ -122,11 +127,16 @@ def tile_picked_andpool_none_e_kernel(tc, xT, w1, offs, out):
 
         sigmoid_unit((0,), 0, FIRST)
         sigmoid_unit((0,), FIRST, V)
+        sigmoid_unit((0,), V, V + 256)
         sigmoid_unit((1,), 0, V, (FIRST,))
-        for product, running, d in ((two, truth, 1), (three, two, 3), (four, three, 2)):
-            for tiles, a, b in (((0,), 0, 256), ((1,), 0, 256), ((0, 1), 256, V)):
-                sigmoid_unit(tiles, d * V + a, d * V + b)
-                multiply(product, running, d, tiles, a, b)
-                if product is four:
+        groups = (((0,), 0, 256, (1, 3, 2)), ((1,), 0, 256, (1, 3, 2)), ((0, 1), 256, V, (3, 1, 2)))
+        chain = (truth, two, three, four)
+        for step in range(3):
+            for tiles, a, b, order in groups:
+                d = order[step]
+                if (step, tiles) != (0, (0,)):
+                    sigmoid_unit(tiles, d * V + a, d * V + b)
+                multiply(chain[step + 1], chain[step], d, tiles, a, b)
+                if step == 2:
                     rows = slice(tiles[0], tiles[-1] + 1)
                     nc.sync.dma_start(out=out_rows[:, rows, a:b], in_=four[:, rows, a:b])

@@ -23,8 +23,9 @@ MT = N // P
 PER_COLUMN = 16
 BANKS = 8
 FIRST = 128
+EARLY = 896
 DIRECT = 640
-HANDED = 448
+HANDED = 416
 SCALAR_CUT = 1280
 
 
@@ -37,29 +38,29 @@ def tile_picked_andpool_none_e_kernel(tc, xT, w1, offs, out):
 
         offsets = keep.tile([P, S // PER_COLUMN], U16, name="offsets")
         planes = [keep.tile([P, T], F32, name=f"plane{j}") for j in range(PACK)]
-        w_raw = [reuse.tile([P, PACK, P], F32, name="w_raw0", align_bytes=64, offset=0), keep.tile([P, PACK, P], F32, name="w_raw1", tag="second", align_bytes=64)]
+        w_raw = [keep.tile([P, PACK, P], F32, name="w_raw0", tag="first", align_bytes=64), reuse.tile([P, PACK, P], F32, name="w_raw1", align_bytes=64, offset=0)]
         x_rows = xT.rearrange("(p j) t -> p j t", j=PACK)
-        nc.sync.dma_start(out=planes[0][:], in_=x_rows[:, 0, :])
+        nc.sync.dma_start(out=planes[2][:], in_=x_rows[:, 2, :])
         nc.sync.dma_start(offsets[:], offs)
-        for j in range(1, PACK):
+        for j in (0, 1, 3):
             nc.sync.dma_start(out=planes[j][:], in_=x_rows[:, j, :])
         w_rows = w1.rearrange("(p j) m -> p j m", j=PACK)
         for m in range(MT):
             nc.sync.dma_start(out=w_raw[m][:], in_=w_rows[:, :, m * P:(m + 1) * P])
 
         warm = keep.tile([P, 1], F32, name="warm")
-        nc.scalar.activation(warm[:], planes[0][:, 0:1], SIGMOID)
+        nc.scalar.activation(warm[:], planes[2][:, 0:1], SIGMOID)
 
         def entries(a, b):
             return offsets[:, a // PER_COLUMN:b // PER_COLUMN]
 
         grouped = keep.tile([P, S, PACK], BF16, name="grouped", align_bytes=64)
         border = DIRECT + HANDED
-        for j in range(PACK - 1):
-            nc.vector.tensor_copy(grouped[:, :border, j], planes[j][:].indirect(entries(0, border)))
-            flat = keep.tile([P, S - border], BF16, name=f"flat{j}")
-            nc.scalar.activation(flat[:], planes[j][:].indirect(entries(border, S)), COPY)
-            nc.scalar.copy(grouped[:, border:, j], flat[:])
+        for j, split in ((2, border), (0, EARLY), (1, EARLY)):
+            nc.vector.tensor_copy(grouped[:, :split, j], planes[j][:].indirect(entries(0, split)))
+            flat = keep.tile([P, S - split], BF16, name=f"flat{j}")
+            nc.scalar.activation(flat[:], planes[j][:].indirect(entries(split, S)), COPY)
+            nc.scalar.copy(grouped[:, split:, j], flat[:])
 
         last = PACK - 1
         nc.vector.tensor_copy(grouped[:, :DIRECT, last], planes[last][:].indirect(entries(0, DIRECT)))
@@ -79,11 +80,11 @@ def tile_picked_andpool_none_e_kernel(tc, xT, w1, offs, out):
         handed = reuse.tile([P, HANDED], BF16, name="handed", align_bytes=64, offset=0)
         nc.scalar.activation(handed[:], planes[last][:].indirect(entries(DIRECT, border)), COPY)
         scales = keep.tile([P, S], U8, name="scales", align_bytes=64)
-        codes_first = reuse.tile([P, DIRECT], U32, name="codes_first", align_bytes=64, offset=896)
-        codes_rest = keep.tile([P, S - DIRECT], U32, name="codes_rest", tag="second", align_bytes=64)
+        codes_first = keep.tile([P, FIRST], U32, name="codes_first", tag="first", align_bytes=64)
+        codes_rest = reuse.tile([P, S - FIRST], U32, name="codes_rest", align_bytes=64, offset=832)
 
         def codes(a, b):
-            return codes_first[:, a:b] if a < DIRECT else codes_rest[:, a - DIRECT:b - DIRECT]
+            return codes_first[:, a:b] if a < FIRST else codes_rest[:, a - FIRST:b - FIRST]
 
         def quantise_entries(a, b):
             nc.vector.quantize_mx(out=codes(a, b).bitcast(FP8X4), scales=scales[:, a:b], in_=grouped[:, a:b, :].rearrange("p e j -> p (e j)"))
@@ -95,9 +96,9 @@ def tile_picked_andpool_none_e_kernel(tc, xT, w1, offs, out):
 
         quantise_w(0)
         quantise_entries(0, FIRST)
+        quantise_w(1)
         quantise_entries(FIRST, V)
         quantise_entries(V, DIRECT)
-        quantise_w(1)
         quantise_entries(3 * V, S)
         nc.vector.tensor_copy(grouped[:, DIRECT:DIRECT + 256, last], handed[:, :256])
         nc.vector.tensor_copy(grouped[:, DIRECT + 256:border, last], handed[:, 256:])
@@ -125,17 +126,15 @@ def tile_picked_andpool_none_e_kernel(tc, xT, w1, offs, out):
             rows = slice(tiles[0], tiles[-1] + 1)
             nc.vector.tensor_tensor(product[:, rows, a:b], running[:, rows, a:b], truth[:, rows, d * V + a:d * V + b], MULT)
 
-        sigmoid_unit((0,), 0, FIRST)
-        sigmoid_unit((0,), FIRST, V)
-        sigmoid_unit((0,), V, V + 256)
-        sigmoid_unit((1,), 0, V, (FIRST,))
+        sigmoid_unit((0, 1), 0, FIRST)
+        for m in range(MT):
+            sigmoid_unit((m,), FIRST, V)
         groups = (((0,), 0, 256, (1, 3, 2)), ((1,), 0, 256, (1, 3, 2)), ((0, 1), 256, V, (3, 1, 2)))
         chain = (truth, two, three, four)
         for step in range(3):
             for tiles, a, b, order in groups:
                 d = order[step]
-                if (step, tiles) != (0, (0,)):
-                    sigmoid_unit(tiles, d * V + a, d * V + b)
+                sigmoid_unit(tiles, d * V + a, d * V + b)
                 multiply(chain[step + 1], chain[step], d, tiles, a, b)
                 if step == 2:
                     rows = slice(tiles[0], tiles[-1] + 1)

@@ -7,6 +7,7 @@ FLOPS = 2 * K * S * N
 
 F32 = mybir.dt.float32
 BF16 = mybir.dt.bfloat16
+I32 = mybir.dt.int32
 U32 = mybir.dt.uint32
 U16 = mybir.dt.uint16
 U8 = mybir.dt.uint8
@@ -23,7 +24,7 @@ MT = N // P
 PER_COLUMN = 16
 BANKS = 8
 FIRST = 128
-EARLY = 896
+EARLY = 640
 DIRECT = 640
 HANDED = 416
 SCALAR_CUT = 1280
@@ -37,37 +38,51 @@ def tile_picked_andpool_none_e_kernel(tc, xT, w1, offs, out):
         psum = ctx.enter_context(tc.psum_pool(name="psum", bufs=1))
 
         offsets = keep.tile([P, S // PER_COLUMN], U16, name="offsets")
-        planes = [keep.tile([P, T], F32, name=f"plane{j}") for j in range(PACK)]
+        first_two = keep.tile([P, 2, T], F32, name="first_two")
+        planes = [first_two[:, 0, :], first_two[:, 1, :]] + [keep.tile([P, T], F32, name=f"plane{j}")[:] for j in range(2, PACK)]
         w_raw = [keep.tile([P, PACK, P], F32, name="w_raw0", tag="first", align_bytes=64), reuse.tile([P, PACK, P], F32, name="w_raw1", align_bytes=64, offset=0)]
         x_rows = xT.rearrange("(p j) t -> p j t", j=PACK)
-        nc.sync.dma_start(out=planes[2][:], in_=x_rows[:, 2, :])
+        nc.sync.dma_start(out=first_two[:], in_=x_rows[:, 0:2, :])
         nc.sync.dma_start(offsets[:], offs)
-        for j in (0, 1, 3):
-            nc.sync.dma_start(out=planes[j][:], in_=x_rows[:, j, :])
+        for j in range(2, PACK):
+            nc.sync.dma_start(out=planes[j], in_=x_rows[:, j, :])
         w_rows = w1.rearrange("(p j) m -> p j m", j=PACK)
         for m in range(MT):
             nc.sync.dma_start(out=w_raw[m][:], in_=w_rows[:, :, m * P:(m + 1) * P])
 
         warm = keep.tile([P, 1], F32, name="warm")
-        nc.scalar.activation(warm[:], planes[2][:, 0:1], SIGMOID)
+        nc.scalar.activation(warm[:], planes[0][:, 0:1], SIGMOID)
 
         def entries(a, b):
             return offsets[:, a // PER_COLUMN:b // PER_COLUMN]
 
         grouped = keep.tile([P, S, PACK], BF16, name="grouped", align_bytes=64)
         border = DIRECT + HANDED
-        for j, split in ((2, border), (0, EARLY), (1, EARLY)):
-            nc.vector.tensor_copy(grouped[:, :split, j], planes[j][:].indirect(entries(0, split)))
-            flat = keep.tile([P, S - split], BF16, name=f"flat{j}")
-            nc.scalar.activation(flat[:], planes[j][:].indirect(entries(split, S)), COPY)
-            nc.scalar.copy(grouped[:, split:, j], flat[:])
+        pair = keep.tile([P, EARLY, 2], BF16, name="pair")
+        flat_two = [keep.tile([P, 2, b - a], F32, name=f"flat_two{a}") for a, b in ((EARLY, border), (border, S))]
+        for j in range(2):
+            nc.vector.tensor_copy(pair[:, :, j], planes[j].indirect(entries(0, EARLY)))
+        for (a, b), flat in zip(((EARLY, border), (border, S)), flat_two):
+            for j in range(2):
+                nc.scalar.activation(flat[:, j, :], planes[j].indirect(entries(a, b)), COPY)
+        words = grouped[:].rearrange("p e j -> p (e j)").bitcast(I32).rearrange("p (e r) -> p e r", r=2)
+        nc.vector.tensor_copy(words[:, :EARLY, 0], pair[:].rearrange("p e h -> p (e h)").bitcast(I32))
+        nc.gpsimd.tensor_scalar(grouped[:, border:, 0:2], flat_two[1][:].rearrange("p j e -> p e j"), 1.0, 0.0, MULT, ADD)
+        nc.scalar.copy(grouped[:, EARLY:border, 0:2], flat_two[0][:].rearrange("p j e -> p e j"))
+        nc.vector.tensor_copy(grouped[:, :border, 2], planes[2].indirect(entries(0, border)))
+        spans = ((SCALAR_CUT, S), (border, SCALAR_CUT))
+        flats = [keep.tile([P, b - a], BF16, name=f"third{a}") for a, b in spans]
+        for (a, b), flat in zip(spans, flats):
+            nc.scalar.activation(flat[:], planes[2].indirect(entries(a, b)), COPY)
+        for (a, b), flat in zip(spans, flats):
+            nc.scalar.copy(grouped[:, a:b, 2], flat[:])
 
         last = PACK - 1
-        nc.vector.tensor_copy(grouped[:, :DIRECT, last], planes[last][:].indirect(entries(0, DIRECT)))
+        nc.vector.tensor_copy(grouped[:, :DIRECT, last], planes[last].indirect(entries(0, DIRECT)))
         spans = ((SCALAR_CUT, S), (border, SCALAR_CUT))
         flats = [keep.tile([P, b - a], BF16, name=f"last{a}") for a, b in spans]
         for (a, b), flat in zip(spans, flats):
-            nc.scalar.activation(flat[:], planes[last][:].indirect(entries(a, b)), COPY)
+            nc.scalar.activation(flat[:], planes[last].indirect(entries(a, b)), COPY)
         for (a, b), flat in zip(spans, flats):
             nc.scalar.copy(grouped[:, a:b, last], flat[:])
 
@@ -78,7 +93,7 @@ def tile_picked_andpool_none_e_kernel(tc, xT, w1, offs, out):
             nc.gpsimd.tensor_scalar(w_grouped[:, m * P:(m + 1) * P, :], w_raw[m][:].rearrange("p j m -> p m j"), 1.0, 0.0, MULT, ADD)
 
         handed = reuse.tile([P, HANDED], BF16, name="handed", align_bytes=64, offset=0)
-        nc.scalar.activation(handed[:], planes[last][:].indirect(entries(DIRECT, border)), COPY)
+        nc.scalar.activation(handed[:], planes[last].indirect(entries(DIRECT, border)), COPY)
         scales = keep.tile([P, S], U8, name="scales", align_bytes=64)
         codes_first = keep.tile([P, FIRST], U32, name="codes_first", tag="first", align_bytes=64)
         codes_rest = reuse.tile([P, S - FIRST], U32, name="codes_rest", align_bytes=64, offset=832)

@@ -26,7 +26,7 @@ BANKS = 8
 FIRST = 128
 EARLY = 640
 DIRECT = 640
-HANDED = 416
+HANDED = 384
 SCALAR_CUT = 1280
 
 
@@ -96,7 +96,7 @@ def tile_picked_andpool_none_e_kernel(tc, xT, w1, offs, out):
         nc.scalar.activation(handed[:], planes[last].indirect(entries(DIRECT, border)), COPY)
         scales = keep.tile([P, S], U8, name="scales", align_bytes=64)
         codes_first = keep.tile([P, FIRST], U32, name="codes_first", tag="first", align_bytes=64)
-        codes_rest = reuse.tile([P, S - FIRST], U32, name="codes_rest", align_bytes=64, offset=832)
+        codes_rest = reuse.tile([P, S - FIRST], U32, name="codes_rest", align_bytes=64, offset=768)
 
         def codes(a, b):
             return codes_first[:, a:b] if a < FIRST else codes_rest[:, a - FIRST:b - FIRST]

@@ -40,15 +40,15 @@ def tile_picked_andpool_none_e_kernel(tc, xT, w1, offs, out):
         offsets = keep.tile([P, S // PER_COLUMN], U16, name="offsets")
         first_two = keep.tile([P, 2, T], F32, name="first_two")
         planes = [first_two[:, 0, :], first_two[:, 1, :]] + [keep.tile([P, T], F32, name=f"plane{j}")[:] for j in range(2, PACK)]
-        w_raw = [keep.tile([P, PACK, P], F32, name="w_raw0", tag="first", align_bytes=64), reuse.tile([P, PACK, P], F32, name="w_raw1", align_bytes=64, offset=0)]
+        w_raw = [keep.tile([P, 2, N], F32, name="w_raw0", tag="first", align_bytes=64), reuse.tile([P, 2, N], F32, name="w_raw1", align_bytes=64, offset=0)]
         x_rows = xT.rearrange("(p j) t -> p j t", j=PACK)
         nc.sync.dma_start(out=first_two[:], in_=x_rows[:, 0:2, :])
         nc.sync.dma_start(offsets[:], offs)
         for j in range(2, PACK):
             nc.sync.dma_start(out=planes[j], in_=x_rows[:, j, :])
         w_rows = w1.rearrange("(p j) m -> p j m", j=PACK)
-        for m in range(MT):
-            nc.sync.dma_start(out=w_raw[m][:], in_=w_rows[:, :, m * P:(m + 1) * P])
+        for h in range(2):
+            nc.sync.dma_start(out=w_raw[h][:], in_=w_rows[:, 2 * h:2 * h + 2, :])
 
         warm = keep.tile([P, 1], F32, name="warm")
         nc.scalar.activation(warm[:], planes[0][:, 0:1], SIGMOID)
@@ -89,8 +89,8 @@ def tile_picked_andpool_none_e_kernel(tc, xT, w1, offs, out):
         w_grouped = keep.tile([P, N, PACK], BF16, name="w_grouped", align_bytes=64)
         w_codes = keep.tile([P, N], U32, name="w_codes", align_bytes=64)
         w_scales = keep.tile([P, N], U8, name="w_scales", align_bytes=64)
-        for m in range(MT):
-            nc.gpsimd.tensor_scalar(w_grouped[:, m * P:(m + 1) * P, :], w_raw[m][:].rearrange("p j m -> p m j"), 1.0, 0.0, MULT, ADD)
+        for h in range(2):
+            nc.gpsimd.tensor_scalar(w_grouped[:, :, 2 * h:2 * h + 2], w_raw[h][:].rearrange("p j m -> p m j"), 1.0, 0.0, MULT, ADD)
 
         handed = reuse.tile([P, HANDED], BF16, name="handed", align_bytes=64, offset=0)
         nc.scalar.activation(handed[:], planes[last].indirect(entries(DIRECT, border)), COPY)

@@ -23,10 +23,10 @@ PIECES = S // V
 MT = N // P
 PER_COLUMN = 16
 BANKS = 8
-FIRST = 128
+FIRST = 256
 EARLY = 640
 DIRECT = 640
-HANDED = 384
+HANDED = 320
 SCALAR_CUT = 1280
 
 
@@ -109,16 +109,14 @@ def tile_picked_andpool_none_e_kernel(tc, xT, w1, offs, out):
             nc.vector.quantize_mx(out=w_codes[:, cols].bitcast(FP8X4), scales=w_scales[:, cols],
                                   in_=w_grouped[:, cols, :].rearrange("p m j -> p (m j)"))
 
-        quantise_w(0)
         quantise_entries(0, FIRST)
+        quantise_w(0)
         quantise_w(1)
-        quantise_entries(FIRST, V)
-        quantise_entries(V, DIRECT)
-        quantise_entries(3 * V, S)
-        nc.vector.tensor_copy(grouped[:, DIRECT:DIRECT + 256, last], handed[:, :256])
-        nc.vector.tensor_copy(grouped[:, DIRECT + 256:border, last], handed[:, 256:])
-        quantise_entries(DIRECT, DIRECT + 256)
-        quantise_entries(DIRECT + 256, 3 * V)
+        quantise_entries(FIRST, DIRECT)
+        quantise_entries(SCALAR_CUT, S)
+        nc.vector.tensor_copy(grouped[:, DIRECT:border, last], handed[:])
+        quantise_entries(1024, SCALAR_CUT)
+        quantise_entries(DIRECT, 1024)
 
         truth = keep.tile([P, MT, S], F32, name="truth")
 
@@ -141,9 +139,9 @@ def tile_picked_andpool_none_e_kernel(tc, xT, w1, offs, out):
             rows = slice(tiles[0], tiles[-1] + 1)
             nc.vector.tensor_tensor(product[:, rows, a:b], running[:, rows, a:b], truth[:, rows, d * V + a:d * V + b], MULT)
 
-        sigmoid_unit((0, 1), 0, FIRST)
         for m in range(MT):
-            sigmoid_unit((m,), FIRST, V)
+            sigmoid_unit((m,), 0, FIRST)
+        sigmoid_unit((0, 1), FIRST, V)
         groups = (((0,), 0, 256, (1, 3, 2)), ((1,), 0, 256, (1, 3, 2)), ((0, 1), 256, V, (3, 1, 2)))
         chain = (truth, two, three, four)
         for step in range(3):

@@ -25,8 +25,8 @@ PER_COLUMN = 16
 BANKS = 8
 FIRST = 256
 EARLY = 640
-DIRECT = 640
-HANDED = 320
+DIRECT = 512
+HANDED = 512
 SCALAR_CUT = 1280
 
 
@@ -40,15 +40,14 @@ def tile_picked_andpool_none_e_kernel(tc, xT, w1, offs, out):
         offsets = keep.tile([P, S // PER_COLUMN], U16, name="offsets")
         first_two = keep.tile([P, 2, T], F32, name="first_two")
         planes = [first_two[:, 0, :], first_two[:, 1, :]] + [keep.tile([P, T], F32, name=f"plane{j}")[:] for j in range(2, PACK)]
-        w_raw = [keep.tile([P, 2, N], F32, name="w_raw0", tag="first", align_bytes=64), reuse.tile([P, 2, N], F32, name="w_raw1", align_bytes=64, offset=0)]
+        w_raw = reuse.tile([P, PACK, N], F32, name="w_raw", align_bytes=64, offset=0)
         x_rows = xT.rearrange("(p j) t -> p j t", j=PACK)
         nc.sync.dma_start(out=first_two[:], in_=x_rows[:, 0:2, :])
         nc.sync.dma_start(offsets[:], offs)
         for j in range(2, PACK):
             nc.sync.dma_start(out=planes[j], in_=x_rows[:, j, :])
         w_rows = w1.rearrange("(p j) m -> p j m", j=PACK)
-        for h in range(2):
-            nc.sync.dma_start(out=w_raw[h][:], in_=w_rows[:, 2 * h:2 * h + 2, :])
+        nc.sync.dma_start(out=w_raw[:], in_=w_rows)
 
         warm = keep.tile([P, 1], F32, name="warm")
         nc.scalar.activation(warm[:], planes[0][:, 0:1], SIGMOID)
@@ -89,17 +88,18 @@ def tile_picked_andpool_none_e_kernel(tc, xT, w1, offs, out):
         w_grouped = keep.tile([P, N, PACK], BF16, name="w_grouped", align_bytes=64)
         w_codes = keep.tile([P, N], U32, name="w_codes", align_bytes=64)
         w_scales = keep.tile([P, N], U8, name="w_scales", align_bytes=64)
-        for h in range(2):
-            nc.gpsimd.tensor_scalar(w_grouped[:, :, 2 * h:2 * h + 2], w_raw[h][:].rearrange("p j m -> p m j"), 1.0, 0.0, MULT, ADD)
+        for m in range(MT):
+            nc.vector.tensor_copy(w_grouped[:, m * P:(m + 1) * P, :].rearrange("p (c i) j -> p c j i", i=4),
+                                  w_raw[:, :, m * P:(m + 1) * P].rearrange("p j (c i) -> p c j i", i=4))
 
         handed = reuse.tile([P, HANDED], BF16, name="handed", align_bytes=64, offset=0)
-        nc.scalar.activation(handed[:], planes[last].indirect(entries(DIRECT, border)), COPY)
+        for a, b in ((DIRECT, 2 * V), (2 * V, border)):
+            nc.scalar.activation(handed[:, a - DIRECT:b - DIRECT], planes[last].indirect(entries(a, b)), COPY)
         scales = keep.tile([P, S], U8, name="scales", align_bytes=64)
-        codes_first = keep.tile([P, FIRST], U32, name="codes_first", tag="first", align_bytes=64)
-        codes_rest = reuse.tile([P, S - FIRST], U32, name="codes_rest", align_bytes=64, offset=768)
+        all_codes = reuse.tile([P, S], U32, name="all_codes", align_bytes=64, offset=1024)
 
         def codes(a, b):
-            return codes_first[:, a:b] if a < FIRST else codes_rest[:, a - FIRST:b - FIRST]
+            return all_codes[:, a:b]
 
         def quantise_entries(a, b):
             nc.vector.quantize_mx(out=codes(a, b).bitcast(FP8X4), scales=scales[:, a:b], in_=grouped[:, a:b, :].rearrange("p e j -> p (e j)"))
@@ -109,14 +109,16 @@ def tile_picked_andpool_none_e_kernel(tc, xT, w1, offs, out):
             nc.vector.quantize_mx(out=w_codes[:, cols].bitcast(FP8X4), scales=w_scales[:, cols],
                                   in_=w_grouped[:, cols, :].rearrange("p m j -> p (m j)"))
 
-        quantise_entries(0, FIRST)
         quantise_w(0)
+        quantise_entries(0, FIRST)
         quantise_w(1)
-        quantise_entries(FIRST, DIRECT)
-        quantise_entries(SCALAR_CUT, S)
-        nc.vector.tensor_copy(grouped[:, DIRECT:border, last], handed[:])
-        quantise_entries(1024, SCALAR_CUT)
-        quantise_entries(DIRECT, 1024)
+        quantise_entries(FIRST, V)
+        quantise_entries(3 * V, S)
+        quantise_entries(border, 3 * V)
+        for a, b in ((DIRECT, 2 * V), (2 * V, border)):
+            nc.vector.tensor_copy(grouped[:, a:b, last], handed[:, a - DIRECT:b - DIRECT])
+        quantise_entries(V, 2 * V)
+        quantise_entries(2 * V, border)
 
         truth = keep.tile([P, MT, S], F32, name="truth")
 
@@ -142,7 +144,7 @@ def tile_picked_andpool_none_e_kernel(tc, xT, w1, offs, out):
         for m in range(MT):
             sigmoid_unit((m,), 0, FIRST)
         sigmoid_unit((0, 1), FIRST, V)
-        groups = (((0,), 0, 256, (1, 3, 2)), ((1,), 0, 256, (1, 3, 2)), ((0, 1), 256, V, (3, 1, 2)))
+        groups = (((0,), 0, 256, (3, 1, 2)), ((1,), 0, 256, (3, 1, 2)), ((0, 1), 256, V, (3, 2, 1)))
         chain = (truth, two, three, four)
         for step in range(3):
             for tiles, a, b, order in groups:

@@ -25,8 +25,8 @@ PER_COLUMN = 16
 BANKS = 8
 FIRST = 256
 EARLY = 640
-DIRECT = 512
-HANDED = 512
+DIRECT = 576
+HANDED = 448
 SCALAR_CUT = 1280
 
 
@@ -144,7 +144,7 @@ def tile_picked_andpool_none_e_kernel(tc, xT, w1, offs, out):
         for m in range(MT):
             sigmoid_unit((m,), 0, FIRST)
         sigmoid_unit((0, 1), FIRST, V)
-        groups = (((0,), 0, 256, (3, 1, 2)), ((1,), 0, 256, (3, 1, 2)), ((0, 1), 256, V, (3, 2, 1)))
+        groups = (((0, 1), 256, V, (3, 2, 1)), ((0,), 0, 256, (3, 1, 2)), ((1,), 0, 256, (3, 1, 2)))
         chain = (truth, two, three, four)
         for step in range(3):
             for tiles, a, b, order in groups:

from contextlib import ExitStack

import concourse.mybir as mybir

K, T, S, V, N = 512, 4096, 1536, 384, 256
FLOPS = 2 * K * S * N

F32 = mybir.dt.float32
BF16 = mybir.dt.bfloat16
I32 = mybir.dt.int32
U32 = mybir.dt.uint32
U16 = mybir.dt.uint16
U8 = mybir.dt.uint8
FP8X4 = mybir.dt.float8_e4m3fn_x4
SIGMOID = mybir.ActivationFunctionType.Sigmoid
COPY = mybir.ActivationFunctionType.Copy
MULT = mybir.AluOpType.mult
ADD = mybir.AluOpType.add

P = 128
PACK = 4
PIECES = S // V
MT = N // P
PER_COLUMN = 16
BANKS = 8
FIRST = 256
EARLY = 640
DIRECT = 576
HANDED = 448
SCALAR_CUT = 1280


def tile_picked_andpool_none_e_kernel(tc, xT, w1, offs, out):
    nc = tc.nc
    with ExitStack() as ctx:
        keep = ctx.enter_context(tc.tile_pool(name="keep", bufs=1))
        reuse = ctx.enter_context(tc.tile_pool(name="reuse", bufs=1))
        psum = ctx.enter_context(tc.psum_pool(name="psum", bufs=1))

        offsets = keep.tile([P, S // PER_COLUMN], U16, name="offsets")
        first_two = keep.tile([P, 2, T], F32, name="first_two")
        planes = [first_two[:, 0, :], first_two[:, 1, :]] + [keep.tile([P, T], F32, name=f"plane{j}")[:] for j in range(2, PACK)]
        w_raw = reuse.tile([P, PACK, N], F32, name="w_raw", align_bytes=64, offset=0)
        x_rows = xT.rearrange("(p j) t -> p j t", j=PACK)
        nc.sync.dma_start(out=first_two[:], in_=x_rows[:, 0:2, :])
        nc.sync.dma_start(offsets[:], offs)
        for j in range(2, PACK):
            nc.sync.dma_start(out=planes[j], in_=x_rows[:, j, :])
        w_rows = w1.rearrange("(p j) m -> p j m", j=PACK)
        nc.sync.dma_start(out=w_raw[:], in_=w_rows)

        warm = keep.tile([P, 1], F32, name="warm")
        nc.scalar.activation(warm[:], planes[0][:, 0:1], SIGMOID)

        def entries(a, b):
            return offsets[:, a // PER_COLUMN:b // PER_COLUMN]

        grouped = keep.tile([P, S, PACK], BF16, name="grouped", align_bytes=64)
        border = DIRECT + HANDED
        pair = keep.tile([P, EARLY, 2], BF16, name="pair")
        flat_two = [keep.tile([P, 2, b - a], F32, name=f"flat_two{a}") for a, b in ((EARLY, border), (border, S))]
        for j in range(2):
            nc.vector.tensor_copy(pair[:, :, j], planes[j].indirect(entries(0, EARLY)))
        for (a, b), flat in zip(((EARLY, border), (border, S)), flat_two):
            for j in range(2):
                nc.scalar.activation(flat[:, j, :], planes[j].indirect(entries(a, b)), COPY)
        words = grouped[:].rearrange("p e j -> p (e j)").bitcast(I32).rearrange("p (e r) -> p e r", r=2)
        nc.vector.tensor_copy(words[:, :EARLY, 0], pair[:].rearrange("p e h -> p (e h)").bitcast(I32))
        nc.gpsimd.tensor_scalar(grouped[:, border:, 0:2], flat_two[1][:].rearrange("p j e -> p e j"), 1.0, 0.0, MULT, ADD)
        nc.scalar.copy(grouped[:, EARLY:border, 0:2], flat_two[0][:].rearrange("p j e -> p e j"))
        nc.vector.tensor_copy(grouped[:, :border, 2], planes[2].indirect(entries(0, border)))
        spans = ((SCALAR_CUT, S), (border, SCALAR_CUT))
        flats = [keep.tile([P, b - a], BF16, name=f"third{a}") for a, b in spans]
        for (a, b), flat in zip(spans, flats):
            nc.scalar.activation(flat[:], planes[2].indirect(entries(a, b)), COPY)
        for (a, b), flat in zip(spans, flats):
            nc.scalar.copy(grouped[:, a:b, 2], flat[:])

        last = PACK - 1
        nc.vector.tensor_copy(grouped[:, :DIRECT, last], planes[last].indirect(entries(0, DIRECT)))
        spans = ((SCALAR_CUT, S), (border, SCALAR_CUT))
        flats = [keep.tile([P, b - a], BF16, name=f"last{a}") for a, b in spans]
        for (a, b), flat in zip(spans, flats):
            nc.scalar.activation(flat[:], planes[last].indirect(entries(a, b)), COPY)
        for (a, b), flat in zip(spans, flats):
            nc.scalar.copy(grouped[:, a:b, last], flat[:])

        w_grouped = keep.tile([P, N, PACK], BF16, name="w_grouped", align_bytes=64)
        w_codes = keep.tile([P, N], U32, name="w_codes", align_bytes=64)
        w_scales = keep.tile([P, N], U8, name="w_scales", align_bytes=64)
        for m in range(MT):
            nc.vector.tensor_copy(w_grouped[:, m * P:(m + 1) * P, :].rearrange("p (c i) j -> p c j i", i=4),
                                  w_raw[:, :, m * P:(m + 1) * P].rearrange("p j (c i) -> p c j i", i=4))

        handed = reuse.tile([P, HANDED], BF16, name="handed", align_bytes=64, offset=0)
        for a, b in ((DIRECT, 2 * V), (2 * V, border)):
            nc.scalar.activation(handed[:, a - DIRECT:b - DIRECT], planes[last].indirect(entries(a, b)), COPY)
        scales = keep.tile([P, S], U8, name="scales", align_bytes=64)
        all_codes = reuse.tile([P, S], U32, name="all_codes", align_bytes=64, offset=1024)

        def codes(a, b):
            return all_codes[:, a:b]

        def quantise_entries(a, b):
            nc.vector.quantize_mx(out=codes(a, b).bitcast(FP8X4), scales=scales[:, a:b], in_=grouped[:, a:b, :].rearrange("p e j -> p (e j)"))

        def quantise_w(m):
            cols = slice(m * P, (m + 1) * P)
            nc.vector.quantize_mx(out=w_codes[:, cols].bitcast(FP8X4), scales=w_scales[:, cols],
                                  in_=w_grouped[:, cols, :].rearrange("p m j -> p (m j)"))

        quantise_w(0)
        quantise_entries(0, FIRST)
        quantise_w(1)
        quantise_entries(FIRST, V)
        quantise_entries(3 * V, S)
        quantise_entries(border, 3 * V)
        for a, b in ((DIRECT, 2 * V), (2 * V, border)):
            nc.vector.tensor_copy(grouped[:, a:b, last], handed[:, a - DIRECT:b - DIRECT])
        quantise_entries(V, 2 * V)
        quantise_entries(2 * V, border)

        truth = keep.tile([P, MT, S], F32, name="truth")

        def sigmoid_unit(tiles, a, b, cuts=()):
            bank = psum.tile([P, len(tiles), b - a], F32, name="bank", bufs=BANKS)
            edges = [a, *cuts, b]
            for i, m in enumerate(tiles):
                cols = slice(m * P, (m + 1) * P)
                for lo, hi in zip(edges, edges[1:]):
                    nc.tensor.matmul_mx(out=bank[:, i, lo - a:hi - a], lhsT=w_codes[:, cols].bitcast(FP8X4), lhsT_scale=w_scales[:, cols],
                                        rhs=codes(lo, hi).bitcast(FP8X4), rhs_scale=scales[:, lo:hi], start=True, stop=True)
            nc.scalar.activation(truth[:, tiles[0]:tiles[-1] + 1, a:b], bank[:], SIGMOID)

        out_rows = out.rearrange("(m p) v -> p m v", p=P)
        two = keep.tile([P, MT, V], F32, name="two")
        three = keep.tile([P, MT, V], F32, name="three")
        four = keep.tile([P, MT, V], F32, name="four")

        def multiply(product, running, d, tiles, a, b):
            rows = slice(tiles[0], tiles[-1] + 1)
            nc.vector.tensor_tensor(product[:, rows, a:b], running[:, rows, a:b], truth[:, rows, d * V + a:d * V + b], MULT)

        for m in range(MT):
            sigmoid_unit((m,), 0, FIRST)
        sigmoid_unit((0, 1), FIRST, V)
        groups = (((0, 1), 256, V, (3, 2, 1)), ((0,), 0, 256, (3, 1, 2)), ((1,), 0, 256, (3, 1, 2)))
        chain = (truth, two, three, four)
        for step in range(3):
            for tiles, a, b, order in groups:
                d = order[step]
                sigmoid_unit(tiles, d * V + a, d * V + b)
                multiply(chain[step + 1], chain[step], d, tiles, a, b)
                if step == 2:
                    rows = slice(tiles[0], tiles[-1] + 1)
                    nc.sync.dma_start(out=out_rows[:, rows, a:b], in_=four[:, rows, a:b])
